import numpy as np
import ml_dtypes


def mxq(x, axis, fmt="e4m3"):
    dtype, down = {"e4m3": (ml_dtypes.float8_e4m3fn, 7), "e5m2": (ml_dtypes.float8_e5m2, 14)}[fmt]
    v = np.moveaxis(np.asarray(x, np.float32).astype(ml_dtypes.bfloat16).astype(np.float64), axis, -1)
    blocks = v.reshape(v.shape[:-1] + (-1, 32))
    amax = np.abs(blocks).max(-1, keepdims=True)
    byte = np.maximum(np.where(amax > 0, np.frexp(amax)[1] - 1 + 127, 0) - down, 1)
    scale = np.exp2(byte - 127.0)
    codes = (blocks / scale).astype(np.float32).astype(dtype).astype(np.float64)
    return np.moveaxis((codes * scale).reshape(v.shape), -1, axis)


WIDE = False


def mx_kscale(k):
    if not WIDE:
        return np.ones(k)
    levels = np.array([10, -10, 5, -5, 0])
    if k % 512:
        return np.exp2(np.random.permutation(np.resize(levels, k // 32))).repeat(32)
    a = np.empty((k // 512, 16))
    for p in range(k // 512):
        a[p, :8] = np.random.permutation(np.resize(levels, 8))
        for g in range(8):
            far = levels[np.abs(levels - a[p, g]) >= 10]
            a[p, g + 8] = far[np.random.randint(len(far))]
    return np.exp2(a.ravel()).repeat(32)


def f64(x):
    return np.asarray(x).astype(np.float64)


def striped(idx):
    return np.tile(idx.reshape(-1, 16).T, (8, 1)).astype(np.uint16)


def unstriped(offs):
    return offs[:16].T.reshape(-1).astype(np.int64)


E2M1 = np.array([0.0, 0.5, 1.0, 1.5, 2.0, 3.0, 4.0, 6.0, -0.0, -0.5, -1.0, -1.5, -2.0, -3.0, -4.0, -6.0])


def pack_weight(w, fmt):
    k, n = w.shape
    w = f64(np.asarray(w, np.float32).astype(ml_dtypes.bfloat16)).reshape(k // 32, 32, n)
    amax = np.abs(w).max(1)
    if fmt == "e4m3":
        byte = np.frexp(amax)[1] - 1 + 127 - 7
    else:
        mant, ex = np.frexp(amax / 6.0)
        byte = np.where(mant > 0.5, ex, ex - 1) + 127
    byte = np.clip(np.where(amax > 0, byte, 1), 1, 254)
    scaled = (w * np.exp2(127.0 - byte)[:, None, :]).reshape(k, n).astype(np.float32)
    by_word = np.ascontiguousarray(scaled.reshape(k // 512, 128, 4, n).transpose(0, 1, 3, 2))
    if fmt == "e4m3":
        words = by_word.astype(ml_dtypes.float8_e4m3fn).view(np.uint8)
    else:
        c = by_word.astype(ml_dtypes.float4_e2m1fn).view(np.uint8) & 0xF
        words = (c[..., 0::2] | (c[..., 1::2] << 4)).reshape(k // 512, 128, 2 * n)
    return np.ascontiguousarray(words), np.ascontiguousarray(byte.astype(np.uint8).reshape(k // 512, 16, n))


def unpack_weight(words, scales, fmt):
    g, _, n = scales.shape
    words = np.ascontiguousarray(words).reshape(g, 128, n, -1)
    if fmt == "e4m3":
        vals = words.view(ml_dtypes.float8_e4m3fn).astype(np.float64)
    else:
        nib = np.empty((g, 128, n, 4), np.uint8)
        nib[..., 0::2] = words & 0xF
        nib[..., 1::2] = words >> 4
        vals = E2M1[nib]
    vals = vals * np.repeat(np.exp2(scales.astype(np.float64) - 127.0), 8, axis=1)[..., None]
    return vals.transpose(0, 1, 3, 2).reshape(g * 512, n)


def gelu(v):
    return 0.5 * v * (1.0 + np.tanh(np.sqrt(2.0 / np.pi) * (v + 0.044715 * v**3)))


def striped8(idx):
    return np.concatenate([v.reshape(-1, 16).T for v in idx]).astype(np.uint16)


def unstriped8(offs):
    return np.stack([offs[16 * g:16 * g + 16].T.reshape(-1) for g in range(8)]).astype(np.int64)


def heads(xT, wgt, idx8):
    k = np.arange(xT.shape[0])
    return wgt[k // 4 % 128] * xT[k[:, None], idx8[k % 512 // 64]]


K, T, S, H, N = 1024, 2048, 1024, 512, 512

def setup_inputs():
    n = np.random.standard_normal
    s = mx_kscale(K)[:, None]
    u = mx_kscale(H)[:, None]
    tab_words, tab_scales = pack_weight(n((K, T)) * s, "e4m3")
    wc_words, wc_scales = pack_weight(0.7 * n((K, H)) / np.sqrt(K) / s, "e2m1")
    return {
        "xT": (n((K, T)) * s).astype(np.float32),
        "wgt": np.repeat(np.random.uniform(0.5, 2.0, (8, S)), 16, axis=0).astype(np.float32),
        "offs2": striped8(np.stack([np.random.permutation(T)[:S] for _ in range(8)])),
        "tab_words": tab_words,
        "tab_scales": tab_scales,
        "offs": striped(np.random.permutation(T)[:S]),
        "wn": (0.7 * n((K, H)) / np.sqrt(K) / s).astype(np.float32),
        "wc_words": wc_words,
        "wc_scales": wc_scales,
        "gain": (np.random.uniform(0.5, 2.0, H) * u[:, 0]).astype(np.float32),
        "wo": (n((H, N)) / np.sqrt(H) / u).astype(np.float32),
    }

def reference(xT, wgt, offs2, tab_words, tab_scales, offs, wn, wc_words, wc_scales, gain, wo):
    xg = heads(f64(xT), f64(wgt), unstriped8(offs2))
    v = unpack_weight(tab_words, tab_scales, "e4m3")[:, unstriped(offs)]
    wc = unpack_weight(wc_words, wc_scales, "e2m1")
    p = mxq(f64(wn), 0, "e4m3").T @ mxq(xg, 0, "e4m3")
    c = wc.T @ v
    d = p - c
    h = f64(gain)[:, None] * (1.0 / (1.0 + d * d))
    return mxq(f64(wo), 0, "e4m3").T @ mxq(h, 0, "e4m3")

@@ -1,0 +1,267 @@
+from contextlib import ExitStack
+
+import concourse.mybir as mybir
+
+K, T, S, H, N = 1024, 2048, 1024, 512, 512
+FLOPS = 2 * S * (2 * K * H + H * N)
+
+F32 = mybir.dt.float32
+BF16 = mybir.dt.bfloat16
+I32 = mybir.dt.int32
+U32 = mybir.dt.uint32
+U16 = mybir.dt.uint16
+U8 = mybir.dt.uint8
+E4M3 = mybir.dt.float8_e4m3fn_x4
+E2M1 = mybir.dt.float4_e2m1fn_x4
+ACT = mybir.ActivationFunctionType
+ALU = mybir.AluOpType
+
+P = 128
+PACK = 4
+PASSES = K // (P * PACK)
+HALF = 512
+HALVES = S // HALF
+RUN = 4
+
+
+def tile_list_cauchy_point_occupancy_kernel(
+    tc, xT, wgt, offs2, tab_words, tab_scales, offs, wn, wc_words, wc_scales, gain, wo, out
+):
+    nc = tc.nc
+    with ExitStack() as ctx:
+        lists = ctx.enter_context(tc.tile_pool(name="lists", bufs=1))
+        keep = ctx.enter_context(tc.tile_pool(name="keep", bufs=1))
+        psum = ctx.enter_context(tc.psum_pool(name="psum", bufs=1))
+
+        def held(shape, dtype, name, **kw):
+            return keep.tile(shape, dtype, name=name, align_bytes=64, **kw)
+
+        idx = lists.tile([P, S // 16], U16, name="idx")
+        idx2 = lists.tile([P, S // 16], U16, name="idx2")
+        tab_sc = held([P, T], U8, "tab_sc")
+        wgt_sb = held([P, S], F32, "wgt_sb")
+        x_sb = [[held([P, T], F32, f"x{a}{i}") for i in range(PACK)] for a in range(PASSES)]
+        tab_sb = [held([P, T], I32, f"tab{a}") for a in range(PASSES)]
+        wn_sb = [held([P, PACK, H], F32, f"wn{a}") for a in range(PASSES)]
+        wo_sb = held([P, PACK, N], F32, "wo_sb")
+        wcw_sb = held([P, PASSES, H // 2], I32, "wcw_sb")
+        wcs_sb = held([P, PASSES, H // 4], I32, "wcs_sb")
+        gain_sb = held([P, PACK, 8], F32, "gain_sb")
+        v_sc = held([P, PASSES, S], U8, "v_sc")
+
+        x_rows = xT.rearrange("(a p i) t -> a i p t", a=PASSES, i=PACK)
+        wn_rows = wn.rearrange("(a p i) h -> a p i h", a=PASSES, i=PACK)
+        wo_rows = wo.rearrange("(s t e) n -> t s e n", t=PACK, e=RUN)
+
+        def load_x(a, i):
+            nc.sync.dma_start(out=x_sb[a][i][:], in_=x_rows[a, i])
+
+        def load_tab(a):
+            nc.sync.dma_start(out=tab_sb[a][:], in_=tab_words[a].rearrange("p t i -> p (t i)").bitcast(I32))
+
+        nc.gpsimd.memset(tab_sc[32:64, :].bitcast(I32), 0)
+        nc.gpsimd.memset(tab_sc[64:128, :].bitcast(I32), 0)
+        nc.vector.memset(wcs_sb[:], 0)
+        nc.vector.memset(v_sc[:].rearrange("p a s -> p (a s)").bitcast(I32), 0)
+
+        def half_list(tile, b):
+            return tile[:, b * HALF // 16 : (b + 1) * HALF // 16]
+
+        sc_rows = held([P, S], U8, "sc_rows")
+
+        def place_scale_rows(a):
+            for quad in range(4):
+                row = 16 * a + 4 * quad
+                nc.gpsimd.dma_start(
+                    out=v_sc[32 * quad : 32 * quad + 4, a, :].bitcast(I32), in_=sc_rows[row : row + 4, :].bitcast(I32)
+                )
+
+        nc.sync.dma_start(out=idx[:], in_=offs)
+        nc.sync.dma_start(out=tab_sc[0:32, :].bitcast(I32), in_=tab_scales.rearrange("a q t -> (a q) t").bitcast(I32))
+        nc.sync.dma_start(out=idx2[:], in_=offs2)
+        nc.sync.dma_start(out=wgt_sb[:], in_=wgt)
+        nc.vector.tensor_copy(out=sc_rows[:], in_=tab_sc[:].indirect(idx[:]))
+        for a in range(PASSES):
+            place_scale_rows(a)
+        wcs_rows = wc_scales.bitcast(I32).rearrange("a q w -> q a w")
+        gain_rows = gain.rearrange("(s t e) -> t s e", t=PACK, e=RUN)
+        for i in range(PACK):
+            load_x(0, i)
+            nc.sync.dma_start(out=wcs_sb[32 * i : 32 * i + 4, :, :], in_=wcs_rows[4 * i : 4 * i + 4])
+        nc.sync.dma_start(out=wcw_sb[:], in_=wc_words.bitcast(I32).rearrange("a p w -> p a w"))
+
+        def load_gain(t):
+            with nc.allow_non_contiguous_dma(reason="one gain value a partition"):
+                nc.sync.dma_start(out=gain_sb[:, t, 0:1], in_=gain_rows[t])
+
+        load_x(1, 0)
+        load_x(1, 1)
+        load_gain(0)
+        nc.sync.dma_start(out=wn_sb[0][:], in_=wn_rows[0])
+        load_gain(1)
+        load_tab(0)
+        load_gain(2)
+        load_x(1, 2)
+        load_gain(3)
+        load_x(1, 3)
+        nc.sync.dma_start(out=wn_sb[1][:], in_=wn_rows[1])
+        load_tab(1)
+        for t in range(PACK):
+            nc.sync.dma_start(out=wo_sb[:, t, :], in_=wo_rows[t])
+
+        def quantise(src, width, name, tag=None):
+            codes = held([P, width], U32, name + "_q", tag=tag or name + "_q")
+            scales = held([P, width], U8, name + "_s")
+            nc.vector.quantize_mx(out=codes[:].bitcast(E4M3), scales=scales[:], in_=src)
+            return codes, scales
+
+        def interleaved(ap):
+            return ap.rearrange("p (c i t) -> p c t i", i=RUN, t=PACK)
+
+        def planes(ap):
+            return ap.rearrange("p t (c i) -> p c t i", i=RUN)
+
+        def picked_tiles(a):
+            return [keep.tile([P, PACK, HALF], F32, name=f"xg{a}{b}", tag="f32x4", bufs=4, align_bytes=64) for b in range(HALVES)]
+
+        def gather_x(a, i, picked):
+            for b in range(HALVES):
+                nc.vector.tensor_tensor(
+                    picked[b][:, i, :],
+                    x_sb[a][i][:].indirect(half_list(idx2, b)),
+                    wgt_sb[:, b * HALF : (b + 1) * HALF],
+                    ALU.mult,
+                )
+
+        def round_x(picked, name, tag=None):
+            rounded = keep.tile([P, PACK * HALF], BF16, name=name + "_b", tag="bf16x4", bufs=4, align_bytes=64)
+            nc.scalar.activation(interleaved(rounded[:]), planes(picked[:]), ACT.Copy, scale=-1.0)
+            return quantise(rounded[:], HALF, name, tag)
+
+        def deal_wn(a, copy):
+            rounded = held([P, PACK * H], BF16, f"wnb{a}")
+            dst = rounded[:].rearrange("p (t s e i) -> p t s i e", t=PACK, e=RUN, i=PACK)
+            src = wn_sb[a][:].rearrange("p i (s t e) -> p t s i e", t=PACK, e=RUN)
+            copy(out=dst, in_=src)
+            return quantise(rounded[:], H, f"wnq{a}")
+
+        d_ps = [[psum.tile([P, HALF], F32, name=f"d{b}{t}", tag=f"bank{b}{t}") for t in range(PACK)] for b in range(HALVES)]
+
+        def neighbours_pass(a, b, wq, xq):
+            for t in range(PACK):
+                cols = slice(t * P, (t + 1) * P)
+                nc.tensor.matmul_mx(
+                    out=d_ps[b][t][:],
+                    lhsT=wq[0][:, cols].bitcast(E4M3),
+                    lhsT_scale=wq[1][:, cols],
+                    rhs=xq[0][:].bitcast(E4M3),
+                    rhs_scale=xq[1][:],
+                    start=(a == 0),
+                    stop=False,
+                )
+
+        xg0 = picked_tiles(0)
+        xg1 = picked_tiles(1)
+        for i in range(PACK):
+            gather_x(0, i, xg0)
+        wc_q = held([P, PASSES, H // 2], I32, "wc_q")
+        wc_s = held([P, PASSES, H // 4], I32, "wc_s")
+        nc.vector.tensor_copy(
+            out=wc_q[:].rearrange("p a (t s w) -> p a t s w", t=PACK, w=2),
+            in_=wcw_sb[:].rearrange("p a (s t w) -> p a t s w", t=PACK, w=2),
+        )
+        nc.vector.tensor_copy(
+            out=wc_s[:].rearrange("p a (t s) -> p a t s", t=PACK),
+            in_=wcs_sb[:].rearrange("p a (s t) -> p a t s", t=PACK),
+        )
+        def centroids_pass(a, b, tag):
+            v_q = held([P, HALF], U32, f"vq{a}{b}", tag=tag)
+            nc.vector.tensor_copy(out=v_q[:], in_=tab_sb[a][:].bitcast(U32).indirect(half_list(idx, b)))
+            for t in range(PACK):
+                nc.tensor.matmul_mx(
+                    out=d_ps[b][t][:],
+                    lhsT=wc_q[:, a, t * P // 2 : (t + 1) * P // 2].bitcast(U8).bitcast(E2M1),
+                    lhsT_scale=wc_s[:, a, t * P // 4 : (t + 1) * P // 4].bitcast(U8),
+                    rhs=v_q[:].bitcast(E4M3),
+                    rhs_scale=v_sc[:, a, b * HALF : (b + 1) * HALF],
+                    start=False,
+                    stop=(a == PASSES - 1),
+                )
+
+        gather_x(1, 0, xg1)
+        gather_x(1, 1, xg1)
+        xq0 = [round_x(xg0[b], f"xq0{b}") for b in range(HALVES)]
+        wq0 = deal_wn(0, nc.scalar.copy)
+        for b in range(HALVES):
+            neighbours_pass(0, b, wq0, xq0[b])
+            centroids_pass(0, b, f"vq0{b}")
+        gather_x(1, 2, xg1)
+        gather_x(1, 3, xg1)
+        inv_gain = held([P, PACK], F32, "inv_gain")
+        nc.vector.reciprocal(inv_gain[:], gain_sb[:, :, 0])
+        wq1 = deal_wn(1, nc.vector.tensor_copy)
+        neighbours_pass(1, 0, wq1, round_x(xg1[0], "xq10"))
+        centroids_pass(1, 0, "vq10")
+        neighbours_pass(1, 1, wq1, round_x(xg1[1], "xq11", "xq10_q"))
+        centroids_pass(1, 1, "vq11")
+
+        wo_b = held([P, PACK * N], BF16, "wo_b")
+        nc.vector.tensor_copy(out=interleaved(wo_b[:]), in_=planes(wo_sb[:]))
+        wo_q, wo_s = quantise(wo_b[:], N, "woq")
+
+        out_rows = out.rearrange("(m p) j -> p m j", p=P)
+
+        def second_stage(b, root, lo, width, square, copies):
+            cols = slice(lo, lo + width)
+            h_b = keep.tile([P, PACK * width], BF16, name=f"hb{b}{lo}", tag="bf16x4", bufs=4, align_bytes=64)
+            square(interleaved(h_b[:]), planes(root[:, :, cols]))
+            h_q, h_s = quantise(h_b[:], width, f"hq{b}{lo}")
+            per_bank = HALF // width
+            staged = held([P, N // P, width], F32, f"o{b}{lo}")
+            for bank in range(N // P // per_bank):
+                tag = f"bank{b}{lo // width * (PACK // per_bank) + bank}"
+                o_ps = psum.tile([P, per_bank, width], F32, name=f"o{b}{lo}{bank}", tag=tag)
+                for u in range(per_bank):
+                    m = bank * per_bank + u
+                    nc.tensor.matmul_mx(
+                        out=o_ps[:, u, :],
+                        lhsT=wo_q[:, m * P : (m + 1) * P].bitcast(E4M3),
+                        lhsT_scale=wo_s[:, m * P : (m + 1) * P],
+                        rhs=h_q[:].bitcast(E4M3),
+                        rhs_scale=h_s[:],
+                        start=True,
+                        stop=True,
+                    )
+                rows = slice(bank * per_bank, (bank + 1) * per_bank)
+                copies[bank % len(copies)](out=staged[:, rows, :], in_=o_ps[:])
+                nc.sync.dma_start(out=out_rows[:, rows, b * HALF + lo : b * HALF + lo + width], in_=staged[:, rows, :])
+
+        def square_vector(dst, src):
+            nc.vector.tensor_tensor(dst, src, src, ALU.mult)
+
+        def square_scalar(dst, src):
+            nc.scalar.activation(dst, src, ACT.Square)
+
+        def inverse_root(root, t, cols):
+            nc.scalar.activation(
+                root[:, t, cols],
+                root[:, t, cols],
+                ACT.Abs_reciprocal_sqrt,
+                bias=inv_gain[:, t : t + 1],
+                scale=inv_gain[:, t : t + 1],
+            )
+
+        roots = [keep.tile([P, PACK, HALF], F32, name=f"root{b}", tag="f32x4", bufs=4, align_bytes=64) for b in range(HALVES)]
+        quarter = HALF // 2
+        for b in range(HALVES):
+            for t in range(PACK):
+                nc.scalar.activation(roots[b][:, t, :], d_ps[b][t][:], ACT.Square)
+            for lo in (0, quarter):
+                for t in range(PACK):
+                    inverse_root(roots[b], t, slice(lo, lo + quarter))
+                if b == 0:
+                    second_stage(b, roots[b], lo, quarter, square_vector, [nc.vector.tensor_copy])
+                elif lo == 0:
+                    second_stage(b, roots[b], lo, quarter, square_vector, [nc.scalar.copy])
+                else:
+                    second_stage(b, roots[b], lo, quarter, square_scalar, [nc.scalar.copy, nc.vector.tensor_copy])

@@ -47,7 +47,7 @@ def tile_list_cauchy_point_occupancy_kernel(
         wcw_sb = held([P, PASSES, H // 2], I32, "wcw_sb")
         wcs_sb = held([P, PASSES, H // 4], I32, "wcs_sb")
         gain_sb = held([P, PACK, 8], F32, "gain_sb")
-        v_sc = held([P, PASSES, S], U8, "v_sc")
+        v_sc = [held([P, S], U8, f"v_sc{a}") for a in range(PASSES)]
 
         x_rows = xT.rearrange("(a p i) t -> a i p t", a=PASSES, i=PACK)
         wn_rows = wn.rearrange("(a p i) h -> a p i h", a=PASSES, i=PACK)
@@ -62,50 +62,55 @@ def tile_list_cauchy_point_occupancy_kernel(
         nc.gpsimd.memset(tab_sc[32:64, :].bitcast(I32), 0)
         nc.gpsimd.memset(tab_sc[64:128, :].bitcast(I32), 0)
         nc.vector.memset(wcs_sb[:], 0)
-        nc.vector.memset(v_sc[:].rearrange("p a s -> p (a s)").bitcast(I32), 0)
+        for a in range(PASSES):
+            nc.vector.memset(v_sc[a][:].bitcast(I32), 0)
+
+        warm = held([P, 2], F32, "warm")
+        nc.vector.memset(warm[:, 0:1], 1.0)
+        nc.scalar.activation(warm[:, 1:2], warm[:, 0:1], ACT.Abs_reciprocal_sqrt)
 
         def half_list(tile, b):
             return tile[:, b * HALF // 16 : (b + 1) * HALF // 16]
 
         sc_rows = held([P, S], U8, "sc_rows")
 
-        def place_scale_rows(a):
-            for quad in range(4):
-                row = 16 * a + 4 * quad
-                nc.gpsimd.dma_start(
-                    out=v_sc[32 * quad : 32 * quad + 4, a, :].bitcast(I32), in_=sc_rows[row : row + 4, :].bitcast(I32)
-                )
+        def place_scale_rows(a, quad):
+            row = 16 * a + 4 * quad
+            nc.sync.dma_start(out=v_sc[a][32 * quad : 32 * quad + 4, :].bitcast(I32), in_=sc_rows[row : row + 4, :].bitcast(I32))
 
         nc.sync.dma_start(out=idx[:], in_=offs)
         nc.sync.dma_start(out=tab_sc[0:32, :].bitcast(I32), in_=tab_scales.rearrange("a q t -> (a q) t").bitcast(I32))
         nc.sync.dma_start(out=idx2[:], in_=offs2)
         nc.sync.dma_start(out=wgt_sb[:], in_=wgt)
         nc.vector.tensor_copy(out=sc_rows[:], in_=tab_sc[:].indirect(idx[:]))
-        for a in range(PASSES):
-            place_scale_rows(a)
         wcs_rows = wc_scales.bitcast(I32).rearrange("a q w -> q a w")
         gain_rows = gain.rearrange("(s t e) -> t s e", t=PACK, e=RUN)
-        for i in range(PACK):
-            load_x(0, i)
-            nc.sync.dma_start(out=wcs_sb[32 * i : 32 * i + 4, :, :], in_=wcs_rows[4 * i : 4 * i + 4])
-        nc.sync.dma_start(out=wcw_sb[:], in_=wc_words.bitcast(I32).rearrange("a p w -> p a w"))
 
-        def load_gain(t):
-            with nc.allow_non_contiguous_dma(reason="one gain value a partition"):
+        def load_wn(a):
+            nc.sync.dma_start(out=wn_sb[a][:], in_=wn_rows[a])
+
+        def load_wc_scales(quad):
+            nc.sync.dma_start(out=wcs_sb[32 * quad : 32 * quad + 4, :, :], in_=wcs_rows[4 * quad : 4 * quad + 4])
+
+        def load_wc_words():
+            nc.sync.dma_start(out=wcw_sb[:], in_=wc_words.bitcast(I32).rearrange("a p w -> p a w"))
+
+        large = [lambda i=i: load_x(0, i) for i in range(PACK)]
+        large.extend([lambda: load_x(1, 0), lambda: load_x(1, 1), lambda: load_wn(0), lambda: load_tab(0)])
+        large.extend([lambda: load_x(1, 2), lambda: load_wn(1), lambda: load_x(1, 3), lambda: load_tab(1)])
+        small = [[], [], [load_wc_words]]
+        for quad in range(4):
+            small.append([lambda quad=quad: load_wc_scales(quad), lambda quad=quad: place_scale_rows(0, quad)])
+        for quad in range(4):
+            small.append([lambda quad=quad: place_scale_rows(1, quad)])
+        small.append([])
+        for big, little in zip(large, small):
+            big()
+            for one in little:
+                one()
+        with nc.allow_non_contiguous_dma(reason="one gain value a partition"):
+            for t in range(PACK):
                 nc.sync.dma_start(out=gain_sb[:, t, 0:1], in_=gain_rows[t])
-
-        load_x(1, 0)
-        load_x(1, 1)
-        load_gain(0)
-        nc.sync.dma_start(out=wn_sb[0][:], in_=wn_rows[0])
-        load_gain(1)
-        load_tab(0)
-        load_gain(2)
-        load_x(1, 2)
-        load_gain(3)
-        load_x(1, 3)
-        nc.sync.dma_start(out=wn_sb[1][:], in_=wn_rows[1])
-        load_tab(1)
         for t in range(PACK):
             nc.sync.dma_start(out=wo_sb[:, t, :], in_=wo_rows[t])
 
@@ -157,7 +162,7 @@ def tile_list_cauchy_point_occupancy_kernel(
                     rhs=xq[0][:].bitcast(E4M3),
                     rhs_scale=xq[1][:],
                     start=(a == 0),
-                    stop=False,
+                    stop=(a == PASSES - 1),
                 )
 
         xg0 = picked_tiles(0)
@@ -183,9 +188,9 @@ def tile_list_cauchy_point_occupancy_kernel(
                     lhsT=wc_q[:, a, t * P // 2 : (t + 1) * P // 2].bitcast(U8).bitcast(E2M1),
                     lhsT_scale=wc_s[:, a, t * P // 4 : (t + 1) * P // 4].bitcast(U8),
                     rhs=v_q[:].bitcast(E4M3),
-                    rhs_scale=v_sc[:, a, b * HALF : (b + 1) * HALF],
+                    rhs_scale=v_sc[a][:, b * HALF : (b + 1) * HALF],
                     start=False,
-                    stop=(a == PASSES - 1),
+                    stop=False,
                 )
 
         gather_x(1, 0, xg1)
@@ -196,14 +201,13 @@ def tile_list_cauchy_point_occupancy_kernel(
             neighbours_pass(0, b, wq0, xq0[b])
             centroids_pass(0, b, f"vq0{b}")
         gather_x(1, 2, xg1)
+        wq1 = deal_wn(1, nc.scalar.copy)
         gather_x(1, 3, xg1)
+        for b in range(HALVES):
+            centroids_pass(1, b, "vq1")
+            neighbours_pass(1, b, wq1, round_x(xg1[b], f"xq1{b}"))
         inv_gain = held([P, PACK], F32, "inv_gain")
         nc.vector.reciprocal(inv_gain[:], gain_sb[:, :, 0])
-        wq1 = deal_wn(1, nc.vector.tensor_copy)
-        neighbours_pass(1, 0, wq1, round_x(xg1[0], "xq10"))
-        centroids_pass(1, 0, "vq10")
-        neighbours_pass(1, 1, wq1, round_x(xg1[1], "xq11", "xq10_q"))
-        centroids_pass(1, 1, "vq11")
 
         wo_b = held([P, PACK * N], BF16, "wo_b")
         nc.vector.tensor_copy(out=interleaved(wo_b[:]), in_=planes(wo_sb[:]))

@@ -69,50 +69,45 @@ def tile_list_cauchy_point_occupancy_kernel(
         nc.vector.memset(warm[:, 0:1], 1.0)
         nc.scalar.activation(warm[:, 1:2], warm[:, 0:1], ACT.Abs_reciprocal_sqrt)
 
-        def half_list(tile, b):
-            return tile[:, b * HALF // 16 : (b + 1) * HALF // 16]
-
         sc_rows = held([P, S], U8, "sc_rows")
-
-        def place_scale_rows(a, quad):
-            row = 16 * a + 4 * quad
-            nc.sync.dma_start(out=v_sc[a][32 * quad : 32 * quad + 4, :].bitcast(I32), in_=sc_rows[row : row + 4, :].bitcast(I32))
 
         nc.sync.dma_start(out=idx[:], in_=offs)
         nc.sync.dma_start(out=tab_sc[0:32, :].bitcast(I32), in_=tab_scales.rearrange("a q t -> (a q) t").bitcast(I32))
         nc.sync.dma_start(out=idx2[:], in_=offs2)
         nc.sync.dma_start(out=wgt_sb[:], in_=wgt)
-        nc.vector.tensor_copy(out=sc_rows[:], in_=tab_sc[:].indirect(idx[:]))
-        wcs_rows = wc_scales.bitcast(I32).rearrange("a q w -> q a w")
-        gain_rows = gain.rearrange("(s t e) -> t s e", t=PACK, e=RUN)
+        wc_scale_rows = wc_scales.bitcast(I32).rearrange("a q w -> q a w")
+        gain_cols = gain.rearrange("(s t e) -> t s e", t=PACK, e=RUN)
 
-        def load_wn(a):
-            nc.sync.dma_start(out=wn_sb[a][:], in_=wn_rows[a])
+        def load_gain(t):
+            with nc.allow_non_contiguous_dma(reason="one gain value a partition"):
+                nc.sync.dma_start(out=gain_sb[:, t, 0:1], in_=gain_cols[t])
 
-        def load_wc_scales(quad):
-            nc.sync.dma_start(out=wcs_sb[32 * quad : 32 * quad + 4, :, :], in_=wcs_rows[4 * quad : 4 * quad + 4])
-
-        def load_wc_words():
-            nc.sync.dma_start(out=wcw_sb[:], in_=wc_words.bitcast(I32).rearrange("a p w -> p a w"))
-
-        large = [lambda i=i: load_x(0, i) for i in range(PACK)]
-        large.extend([lambda: load_x(1, 0), lambda: load_x(1, 1), lambda: load_wn(0), lambda: load_tab(0)])
-        large.extend([lambda: load_x(1, 2), lambda: load_wn(1), lambda: load_x(1, 3), lambda: load_tab(1)])
-        small = [[], [], [load_wc_words]]
-        for quad in range(4):
-            small.append([lambda quad=quad: load_wc_scales(quad), lambda quad=quad: place_scale_rows(0, quad)])
-        for quad in range(4):
-            small.append([lambda quad=quad: place_scale_rows(1, quad)])
-        small.append([])
-        for big, little in zip(large, small):
-            big()
-            for one in little:
-                one()
-        with nc.allow_non_contiguous_dma(reason="one gain value a partition"):
-            for t in range(PACK):
-                nc.sync.dma_start(out=gain_sb[:, t, 0:1], in_=gain_rows[t])
+        for i in range(PACK):
+            load_x(0, i)
+            nc.sync.dma_start(out=wcs_sb[32 * i : 32 * i + 4, :, :], in_=wc_scale_rows[4 * i : 4 * i + 4])
+        nc.sync.dma_start(out=wcw_sb[:], in_=wc_words.bitcast(I32).rearrange("a p w -> p a w"))
+        load_x(1, 0)
+        load_x(1, 1)
+        load_gain(0)
+        nc.sync.dma_start(out=wn_sb[0][:], in_=wn_rows[0])
+        load_gain(1)
+        load_x(1, 2)
+        load_gain(2)
+        load_x(1, 3)
+        load_gain(3)
+        nc.sync.dma_start(out=wn_sb[1][:], in_=wn_rows[1])
+        load_tab(0)
+        load_tab(1)
         for t in range(PACK):
             nc.sync.dma_start(out=wo_sb[:, t, :], in_=wo_rows[t])
+
+        nc.vector.tensor_copy(out=sc_rows[:], in_=tab_sc[:].indirect(idx[:]))
+        for a in range(PASSES):
+            for quad in range(4):
+                row = 16 * a + 4 * quad
+                nc.gpsimd.dma_start(
+                    out=v_sc[a][32 * quad : 32 * quad + 4, :].bitcast(I32), in_=sc_rows[row : row + 4, :].bitcast(I32)
+                )
 
         def quantise(src, width, name, tag=None):
             codes = held([P, width], U32, name + "_q", tag=tag or name + "_q")
@@ -126,25 +121,24 @@ def tile_list_cauchy_point_occupancy_kernel(
         def planes(ap):
             return ap.rearrange("p t (c i) -> p c t i", i=RUN)
 
-        def picked_tiles(a):
-            return [keep.tile([P, PACK, HALF], F32, name=f"xg{a}{b}", tag="f32x4", bufs=4, align_bytes=64) for b in range(HALVES)]
+        def list_part(tile, lo, width):
+            return tile[:, lo // 16 : (lo + width) // 16]
 
-        def gather_x(a, i, picked):
-            for b in range(HALVES):
-                nc.vector.tensor_tensor(
-                    picked[b][:, i, :],
-                    x_sb[a][i][:].indirect(half_list(idx2, b)),
-                    wgt_sb[:, b * HALF : (b + 1) * HALF],
-                    ALU.mult,
-                )
+        def gather_x(a, i, picked, lo, width):
+            nc.vector.tensor_tensor(
+                picked[:, i, lo : lo + width],
+                x_sb[a][i][:].indirect(list_part(idx2, lo, width)),
+                wgt_sb[:, lo : lo + width],
+                ALU.mult,
+            )
 
-        def round_x(picked, name, tag=None):
-            rounded = keep.tile([P, PACK * HALF], BF16, name=name + "_b", tag="bf16x4", bufs=4, align_bytes=64)
-            nc.scalar.activation(interleaved(rounded[:]), planes(picked[:]), ACT.Copy, scale=-1.0)
-            return quantise(rounded[:], HALF, name, tag)
+        def round_x(picked, lo, width, name, tag=None):
+            rounded = held([P, PACK * width], BF16, name + "_b")
+            nc.scalar.activation(interleaved(rounded[:]), planes(picked[:, :, lo : lo + width]), ACT.Copy, scale=-1.0)
+            return quantise(rounded[:], width, name, tag)
 
         def deal_wn(a, copy):
-            rounded = held([P, PACK * H], BF16, f"wnb{a}")
+            rounded = held([P, PACK * H], BF16, f"wnb{a}", tag="w_b")
             dst = rounded[:].rearrange("p (t s e i) -> p t s i e", t=PACK, e=RUN, i=PACK)
             src = wn_sb[a][:].rearrange("p i (s t e) -> p t s i e", t=PACK, e=RUN)
             copy(out=dst, in_=src)
@@ -152,23 +146,22 @@ def tile_list_cauchy_point_occupancy_kernel(
 
         d_ps = [[psum.tile([P, HALF], F32, name=f"d{b}{t}", tag=f"bank{b}{t}") for t in range(PACK)] for b in range(HALVES)]
 
-        def neighbours_pass(a, b, wq, xq):
+        def neighbours_pass(a, b, wq, x_q, x_s, stop):
             for t in range(PACK):
                 cols = slice(t * P, (t + 1) * P)
                 nc.tensor.matmul_mx(
                     out=d_ps[b][t][:],
                     lhsT=wq[0][:, cols].bitcast(E4M3),
                     lhsT_scale=wq[1][:, cols],
-                    rhs=xq[0][:].bitcast(E4M3),
-                    rhs_scale=xq[1][:],
+                    rhs=x_q.bitcast(E4M3),
+                    rhs_scale=x_s,
                     start=(a == 0),
-                    stop=(a == PASSES - 1),
+                    stop=stop,
                 )
 
-        xg0 = picked_tiles(0)
-        xg1 = picked_tiles(1)
+        xg = [keep.tile([P, PACK, S], F32, name=f"xg{a}", tag="f32x4", bufs=2, align_bytes=64) for a in range(PASSES)]
         for i in range(PACK):
-            gather_x(0, i, xg0)
+            gather_x(0, i, xg[0], 0, S)
         wc_q = held([P, PASSES, H // 2], I32, "wc_q")
         wc_s = held([P, PASSES, H // 4], I32, "wc_s")
         nc.vector.tensor_copy(
@@ -179,54 +172,99 @@ def tile_list_cauchy_point_occupancy_kernel(
             out=wc_s[:].rearrange("p a (t s) -> p a t s", t=PACK),
             in_=wcs_sb[:].rearrange("p a (s t) -> p a t s", t=PACK),
         )
-        def centroids_pass(a, b, tag):
-            v_q = held([P, HALF], U32, f"vq{a}{b}", tag=tag)
-            nc.vector.tensor_copy(out=v_q[:], in_=tab_sb[a][:].bitcast(U32).indirect(half_list(idx, b)))
+
+        def gather_words(a, lo, width, name):
+            v_q = held([P, width], U32, name)
+            nc.vector.tensor_copy(out=v_q[:], in_=tab_sb[a][:].bitcast(U32).indirect(list_part(idx, lo, width)))
+            return v_q
+
+        def centroids_pass(a, b, v_q, stop):
             for t in range(PACK):
                 nc.tensor.matmul_mx(
                     out=d_ps[b][t][:],
                     lhsT=wc_q[:, a, t * P // 2 : (t + 1) * P // 2].bitcast(U8).bitcast(E2M1),
                     lhsT_scale=wc_s[:, a, t * P // 4 : (t + 1) * P // 4].bitcast(U8),
-                    rhs=v_q[:].bitcast(E4M3),
+                    rhs=v_q.bitcast(E4M3),
                     rhs_scale=v_sc[a][:, b * HALF : (b + 1) * HALF],
                     start=False,
-                    stop=False,
+                    stop=stop,
                 )
 
-        gather_x(1, 0, xg1)
-        gather_x(1, 1, xg1)
-        xq0 = [round_x(xg0[b], f"xq0{b}") for b in range(HALVES)]
+        halves = [slice(b * HALF, (b + 1) * HALF) for b in range(HALVES)]
+        gather_x(1, 0, xg[1], 0, S)
+        gather_x(1, 1, xg[1], 0, S)
+        x_q, x_s = round_x(xg[0], 0, S, "xq0")
         wq0 = deal_wn(0, nc.scalar.copy)
         for b in range(HALVES):
-            neighbours_pass(0, b, wq0, xq0[b])
-            centroids_pass(0, b, f"vq0{b}")
-        gather_x(1, 2, xg1)
+            neighbours_pass(0, b, wq0, x_q[:, halves[b]], x_s[:, halves[b]], False)
+        gather_x(1, 2, xg[1], 0, S)
+        gather_x(1, 3, xg[1], 0, HALF)
+        gather_x(1, 3, xg[1], HALF, HALF)
+        x_q, x_s = round_x(xg[1], 0, HALF, "xq10")
         wq1 = deal_wn(1, nc.scalar.copy)
-        gather_x(1, 3, xg1)
+        v_q = gather_words(0, 0, S, "vq0")
         for b in range(HALVES):
-            centroids_pass(1, b, "vq1")
-            neighbours_pass(1, b, wq1, round_x(xg1[b], f"xq1{b}"))
+            centroids_pass(0, b, v_q[:, halves[b]], False)
+        neighbours_pass(1, 0, wq1, x_q[:], x_s[:], False)
+        centroids_pass(1, 0, gather_words(1, 0, HALF, "vq10")[:], True)
+        centroids_pass(1, 1, gather_words(1, HALF, HALF, "vq11")[:], False)
+        x_q, x_s = round_x(xg[1], HALF, HALF, "xq11", "vq10")
+        neighbours_pass(1, 1, wq1, x_q[:], x_s[:], True)
         inv_gain = held([P, PACK], F32, "inv_gain")
         nc.vector.reciprocal(inv_gain[:], gain_sb[:, :, 0])
 
-        wo_b = held([P, PACK * N], BF16, "wo_b")
+        wo_b = held([P, PACK * N], BF16, "wo_b", tag="w_b")
         nc.vector.tensor_copy(out=interleaved(wo_b[:]), in_=planes(wo_sb[:]))
         wo_q, wo_s = quantise(wo_b[:], N, "woq")
 
         out_rows = out.rearrange("(m p) j -> p m j", p=P)
 
-        def second_stage(b, root, lo, width, square, copies):
-            cols = slice(lo, lo + width)
-            h_b = keep.tile([P, PACK * width], BF16, name=f"hb{b}{lo}", tag="bf16x4", bufs=4, align_bytes=64)
-            square(interleaved(h_b[:]), planes(root[:, :, cols]))
+        def square_vector(dst, src):
+            nc.vector.tensor_tensor(dst, src, src, ALU.mult)
+
+        def square_scalar(dst, src):
+            nc.scalar.activation(dst, src, ACT.Square)
+
+        vec, sca = nc.vector.tensor_copy, nc.scalar.copy
+        width = HALF // 2
+        units = [
+            (0, 0, [square_vector], [(0, vec), (1, vec)]),
+            (0, width, [square_vector], [(2, vec), (3, vec)]),
+            (1, 0, [square_vector], [(0, sca), (1, sca)]),
+            (1, width, [square_scalar, square_vector], [(2, sca), (3, vec)]),
+        ]
+        roots = []
+        for b, lo, squares, banks in units:
+            if lo == 0:
+                d_sq = keep.tile([P, PACK, HALF], F32, name=f"dsq{b}", tag="f32x4", bufs=2, align_bytes=64)
+                for t in range(PACK):
+                    nc.scalar.activation(d_sq[:, t, :], d_ps[b][t][:], ACT.Square)
+            root = held([P, PACK, width], F32, f"root{b}{lo}", tag=f"x0{len(roots)}")
+            for t in range(PACK):
+                nc.scalar.activation(
+                    root[:, t, :],
+                    d_sq[:, t, lo : lo + width],
+                    ACT.Abs_reciprocal_sqrt,
+                    bias=inv_gain[:, t : t + 1],
+                    scale=inv_gain[:, t : t + 1],
+                )
+            roots.append(root)
+
+        results = []
+        for root, (b, lo, squares, banks) in zip(roots, units):
+            h_b = held([P, PACK * width], BF16, f"hb{b}{lo}")
+            share = width // len(squares)
+            for part, square in enumerate(squares):
+                square(
+                    interleaved(h_b[:, PACK * part * share : PACK * (part + 1) * share]),
+                    planes(root[:, :, part * share : (part + 1) * share]),
+                )
             h_q, h_s = quantise(h_b[:], width, f"hq{b}{lo}")
-            per_bank = HALF // width
-            staged = held([P, N // P, width], F32, f"o{b}{lo}")
-            for bank in range(N // P // per_bank):
-                tag = f"bank{b}{lo // width * (PACK // per_bank) + bank}"
-                o_ps = psum.tile([P, per_bank, width], F32, name=f"o{b}{lo}{bank}", tag=tag)
+            per_bank = N // P // len(banks)
+            for place, (bank, copy) in enumerate(banks):
+                o_ps = psum.tile([P, per_bank, width], F32, name=f"o{b}{bank}", tag=f"bank{b}{bank}")
                 for u in range(per_bank):
-                    m = bank * per_bank + u
+                    m = place * per_bank + u
                     nc.tensor.matmul_mx(
                         out=o_ps[:, u, :],
                         lhsT=wo_q[:, m * P : (m + 1) * P].bitcast(E4M3),
@@ -236,36 +274,10 @@ def tile_list_cauchy_point_occupancy_kernel(
                         start=True,
                         stop=True,
                     )
-                rows = slice(bank * per_bank, (bank + 1) * per_bank)
-                copies[bank % len(copies)](out=staged[:, rows, :], in_=o_ps[:])
-                nc.sync.dma_start(out=out_rows[:, rows, b * HALF + lo : b * HALF + lo + width], in_=staged[:, rows, :])
+                rows = slice(place * per_bank, (place + 1) * per_bank)
+                results.append((o_ps, copy, out_rows[:, rows, b * HALF + lo : b * HALF + lo + width], [P, per_bank, width]))
 
-        def square_vector(dst, src):
-            nc.vector.tensor_tensor(dst, src, src, ALU.mult)
-
-        def square_scalar(dst, src):
-            nc.scalar.activation(dst, src, ACT.Square)
-
-        def inverse_root(root, t, cols):
-            nc.scalar.activation(
-                root[:, t, cols],
-                root[:, t, cols],
-                ACT.Abs_reciprocal_sqrt,
-                bias=inv_gain[:, t : t + 1],
-                scale=inv_gain[:, t : t + 1],
-            )
-
-        roots = [keep.tile([P, PACK, HALF], F32, name=f"root{b}", tag="f32x4", bufs=4, align_bytes=64) for b in range(HALVES)]
-        quarter = HALF // 2
-        for b in range(HALVES):
-            for t in range(PACK):
-                nc.scalar.activation(roots[b][:, t, :], d_ps[b][t][:], ACT.Square)
-            for lo in (0, quarter):
-                for t in range(PACK):
-                    inverse_root(roots[b], t, slice(lo, lo + quarter))
-                if b == 0:
-                    second_stage(b, roots[b], lo, quarter, square_vector, [nc.vector.tensor_copy])
-                elif lo == 0:
-                    second_stage(b, roots[b], lo, quarter, square_vector, [nc.scalar.copy])
-                else:
-                    second_stage(b, roots[b], lo, quarter, square_scalar, [nc.scalar.copy, nc.vector.tensor_copy])
+        for number, (o_ps, copy, dest, shape) in enumerate(results):
+            staged = held(shape, F32, f"staged{number}")
+            copy(out=staged[:], in_=o_ps[:])
+            nc.sync.dma_start(out=dest, in_=staged[:])

@@ -75,37 +75,33 @@ def tile_list_cauchy_point_occupancy_kernel(
         nc.sync.dma_start(out=tab_sc[0:32, :].bitcast(I32), in_=tab_scales.rearrange("a q t -> (a q) t").bitcast(I32))
         nc.sync.dma_start(out=idx2[:], in_=offs2)
         nc.sync.dma_start(out=wgt_sb[:], in_=wgt)
-        wc_scale_rows = wc_scales.bitcast(I32).rearrange("a q w -> q a w")
-        gain_cols = gain.rearrange("(s t e) -> t s e", t=PACK, e=RUN)
-
-        def load_gain(t):
-            with nc.allow_non_contiguous_dma(reason="one gain value a partition"):
-                nc.sync.dma_start(out=gain_sb[:, t, 0:1], in_=gain_cols[t])
-
         for i in range(PACK):
             load_x(0, i)
-            nc.sync.dma_start(out=wcs_sb[32 * i : 32 * i + 4, :, :], in_=wc_scale_rows[4 * i : 4 * i + 4])
         nc.sync.dma_start(out=wcw_sb[:], in_=wc_words.bitcast(I32).rearrange("a p w -> p a w"))
         load_x(1, 0)
         load_x(1, 1)
-        load_gain(0)
         nc.sync.dma_start(out=wn_sb[0][:], in_=wn_rows[0])
-        load_gain(1)
-        load_x(1, 2)
-        load_gain(2)
-        load_x(1, 3)
-        load_gain(3)
-        nc.sync.dma_start(out=wn_sb[1][:], in_=wn_rows[1])
         load_tab(0)
+        load_x(1, 2)
+        load_x(1, 3)
+        nc.sync.dma_start(out=wn_sb[1][:], in_=wn_rows[1])
         load_tab(1)
         for t in range(PACK):
             nc.sync.dma_start(out=wo_sb[:, t, :], in_=wo_rows[t])
+
+        gain_cols = gain.rearrange("(s t e) -> t s e", t=PACK, e=RUN)
+        with nc.allow_non_contiguous_dma(reason="one gain value a partition"):
+            for t in range(PACK):
+                nc.gpsimd.dma_start(out=gain_sb[:, t, 0:1], in_=gain_cols[t])
+        wc_scale_rows = wc_scales.bitcast(I32).rearrange("a q w -> q a w")
+        for quad in range(4):
+            nc.scalar.dma_start(out=wcs_sb[32 * quad : 32 * quad + 4, :, :], in_=wc_scale_rows[4 * quad : 4 * quad + 4])
 
         nc.vector.tensor_copy(out=sc_rows[:], in_=tab_sc[:].indirect(idx[:]))
         for a in range(PASSES):
             for quad in range(4):
                 row = 16 * a + 4 * quad
-                nc.gpsimd.dma_start(
+                nc.scalar.dma_start(
                     out=v_sc[a][32 * quad : 32 * quad + 4, :].bitcast(I32), in_=sc_rows[row : row + 4, :].bitcast(I32)
                 )
 
@@ -116,10 +112,10 @@ def tile_list_cauchy_point_occupancy_kernel(
             return codes, scales
 
         def interleaved(ap):
-            return ap.rearrange("p (c i t) -> p c t i", i=RUN, t=PACK)
+            return ap.rearrange("p (c i t) -> p c t i", i=2, t=PACK)
 
         def planes(ap):
-            return ap.rearrange("p t (c i) -> p c t i", i=RUN)
+            return ap.rearrange("p t (c i) -> p c t i", i=2)
 
         def list_part(tile, lo, width):
             return tile[:, lo // 16 : (lo + width) // 16]
@@ -195,22 +191,21 @@ def tile_list_cauchy_point_occupancy_kernel(
         gather_x(1, 1, xg[1], 0, S)
         x_q, x_s = round_x(xg[0], 0, S, "xq0")
         wq0 = deal_wn(0, nc.scalar.copy)
+        v_q = gather_words(0, 0, S, "vq0")
         for b in range(HALVES):
             neighbours_pass(0, b, wq0, x_q[:, halves[b]], x_s[:, halves[b]], False)
+            centroids_pass(0, b, v_q[:, halves[b]], False)
         gather_x(1, 2, xg[1], 0, S)
         gather_x(1, 3, xg[1], 0, HALF)
         gather_x(1, 3, xg[1], HALF, HALF)
+        wq1 = deal_wn(1, nc.vector.tensor_copy)
         x_q, x_s = round_x(xg[1], 0, HALF, "xq10")
-        wq1 = deal_wn(1, nc.scalar.copy)
-        v_q = gather_words(0, 0, S, "vq0")
-        for b in range(HALVES):
-            centroids_pass(0, b, v_q[:, halves[b]], False)
         neighbours_pass(1, 0, wq1, x_q[:], x_s[:], False)
         centroids_pass(1, 0, gather_words(1, 0, HALF, "vq10")[:], True)
         centroids_pass(1, 1, gather_words(1, HALF, HALF, "vq11")[:], False)
-        x_q, x_s = round_x(xg[1], HALF, HALF, "xq11", "vq10")
+        x_q, x_s = round_x(xg[1], HALF, HALF, "xq11", "xq10_q")
         neighbours_pass(1, 1, wq1, x_q[:], x_s[:], True)
-        inv_gain = held([P, PACK], F32, "inv_gain")
+        inv_gain = held([P, PACK], F32, "inv_gain", tag="x12")
         nc.vector.reciprocal(inv_gain[:], gain_sb[:, :, 0])
 
         wo_b = held([P, PACK * N], BF16, "wo_b", tag="w_b")
@@ -226,20 +221,21 @@ def tile_list_cauchy_point_occupancy_kernel(
             nc.scalar.activation(dst, src, ACT.Square)
 
         vec, sca = nc.vector.tensor_copy, nc.scalar.copy
-        width = HALF // 2
         units = [
-            (0, 0, [square_vector], [(0, vec), (1, vec)]),
-            (0, width, [square_vector], [(2, vec), (3, vec)]),
-            (1, 0, [square_vector], [(0, sca), (1, sca)]),
-            (1, width, [square_scalar, square_vector], [(2, sca), (3, vec)]),
+            (0, 0, 256, square_vector, [(0, vec), (1, vec)]),
+            (0, 256, 256, square_vector, [(2, vec), (3, vec)]),
+            (1, 0, 256, square_vector, [(0, sca), (1, sca)]),
+            (1, 256, 128, square_vector, [(2, vec)]),
+            (1, 384, 128, square_scalar, [(3, sca)]),
         ]
         roots = []
-        for b, lo, squares, banks in units:
+        x_tags = [f"x{a}{i}" for a in range(PASSES) for i in range(PACK)]
+        for b, lo, width, square, banks in units:
             if lo == 0:
                 d_sq = keep.tile([P, PACK, HALF], F32, name=f"dsq{b}", tag="f32x4", bufs=2, align_bytes=64)
                 for t in range(PACK):
                     nc.scalar.activation(d_sq[:, t, :], d_ps[b][t][:], ACT.Square)
-            root = held([P, PACK, width], F32, f"root{b}{lo}", tag=f"x0{len(roots)}")
+            root = held([P, PACK, width], F32, f"root{b}{lo}", tag=x_tags[len(roots)])
             for t in range(PACK):
                 nc.scalar.activation(
                     root[:, t, :],
@@ -251,14 +247,9 @@ def tile_list_cauchy_point_occupancy_kernel(
             roots.append(root)
 
         results = []
-        for root, (b, lo, squares, banks) in zip(roots, units):
+        for root, (b, lo, width, square, banks) in zip(roots, units):
             h_b = held([P, PACK * width], BF16, f"hb{b}{lo}")
-            share = width // len(squares)
-            for part, square in enumerate(squares):
-                square(
-                    interleaved(h_b[:, PACK * part * share : PACK * (part + 1) * share]),
-                    planes(root[:, :, part * share : (part + 1) * share]),
-                )
+            square(interleaved(h_b[:]), planes(root[:]))
             h_q, h_s = quantise(h_b[:], width, f"hq{b}{lo}")
             per_bank = N // P // len(banks)
             for place, (bank, copy) in enumerate(banks):

@@ -19,8 +19,9 @@ ALU = mybir.AluOpType
 P = 128
 PACK = 4
 PASSES = K // (P * PACK)
-HALF = 512
-HALVES = S // HALF
+CHUNK = 256
+CHUNKS = S // CHUNK
+FP4_N = 128
 RUN = 4
 
 
@@ -31,10 +32,11 @@ def tile_list_cauchy_point_occupancy_kernel(
     with ExitStack() as ctx:
         lists = ctx.enter_context(tc.tile_pool(name="lists", bufs=1))
         keep = ctx.enter_context(tc.tile_pool(name="keep", bufs=1))
+        late = ctx.enter_context(tc.tile_pool(name="late", bufs=1))
         psum = ctx.enter_context(tc.psum_pool(name="psum", bufs=1))
 
-        def held(shape, dtype, name, **kw):
-            return keep.tile(shape, dtype, name=name, align_bytes=64, **kw)
+        def held(shape, dtype, name, tag=None):
+            return keep.tile(shape, dtype, name=name, tag=tag or name, align_bytes=64)
 
         idx = lists.tile([P, S // 16], U16, name="idx")
         idx2 = lists.tile([P, S // 16], U16, name="idx2")
@@ -48,6 +50,8 @@ def tile_list_cauchy_point_occupancy_kernel(
         wcs_sb = held([P, PASSES, H // 4], I32, "wcs_sb")
         gain_sb = held([P, PACK, 8], F32, "gain_sb")
         v_sc = [held([P, S], U8, f"v_sc{a}") for a in range(PASSES)]
+        rest = S - CHUNK
+        sc_rows = late.tile([P, S], U8, name="sc_rows", offset=4 * rest - S // 2, align_bytes=64)
 
         x_rows = xT.rearrange("(a p i) t -> a i p t", a=PASSES, i=PACK)
         wn_rows = wn.rearrange("(a p i) h -> a p i h", a=PASSES, i=PACK)
@@ -59,8 +63,8 @@ def tile_list_cauchy_point_occupancy_kernel(
         def load_tab(a):
             nc.sync.dma_start(out=tab_sb[a][:], in_=tab_words[a].rearrange("p t i -> p (t i)").bitcast(I32))
 
-        nc.gpsimd.memset(tab_sc[32:64, :].bitcast(I32), 0)
-        nc.gpsimd.memset(tab_sc[64:128, :].bitcast(I32), 0)
+        nc.vector.memset(tab_sc[32:64, :].bitcast(I32), 0)
+        nc.vector.memset(tab_sc[64:128, :].bitcast(I32), 0)
         nc.vector.memset(wcs_sb[:], 0)
         for a in range(PASSES):
             nc.vector.memset(v_sc[a][:].bitcast(I32), 0)
@@ -69,23 +73,42 @@ def tile_list_cauchy_point_occupancy_kernel(
         nc.vector.memset(warm[:, 0:1], 1.0)
         nc.scalar.activation(warm[:, 1:2], warm[:, 0:1], ACT.Abs_reciprocal_sqrt)
 
-        sc_rows = held([P, S], U8, "sc_rows")
-
         nc.sync.dma_start(out=idx[:], in_=offs)
         nc.sync.dma_start(out=tab_sc[0:32, :].bitcast(I32), in_=tab_scales.rearrange("a q t -> (a q) t").bitcast(I32))
         nc.sync.dma_start(out=idx2[:], in_=offs2)
         nc.sync.dma_start(out=wgt_sb[:], in_=wgt)
         for i in range(PACK):
             load_x(0, i)
-        nc.sync.dma_start(out=wcw_sb[:], in_=wc_words.bitcast(I32).rearrange("a p w -> p a w"))
-        load_x(1, 0)
-        load_x(1, 1)
-        nc.sync.dma_start(out=wn_sb[0][:], in_=wn_rows[0])
-        load_tab(0)
-        load_x(1, 2)
-        load_x(1, 3)
-        nc.sync.dma_start(out=wn_sb[1][:], in_=wn_rows[1])
-        load_tab(1)
+
+        nc.vector.tensor_copy(out=sc_rows[:], in_=tab_sc[:].indirect(idx[:]))
+
+        def move_scales(a, quad):
+            row = 16 * a + 4 * quad
+            nc.sync.dma_start(
+                out=v_sc[a][32 * quad : 32 * quad + 4, :].bitcast(I32), in_=sc_rows[row : row + 4, :].bitcast(I32)
+            )
+
+        def load_wn(a):
+            nc.sync.dma_start(out=wn_sb[a][:], in_=wn_rows[a])
+
+        def load_wc():
+            nc.sync.dma_start(out=wcw_sb[:], in_=wc_words.bitcast(I32).rearrange("a p w -> p a w"))
+
+        big_loads = [
+            lambda: load_x(1, 0),
+            lambda: load_x(1, 1),
+            lambda: load_x(1, 2),
+            load_wc,
+            lambda: load_wn(0),
+            lambda: load_wn(1),
+            lambda: load_x(1, 3),
+            lambda: load_tab(0),
+            lambda: load_tab(1),
+        ]
+        for number, load in enumerate(big_loads):
+            load()
+            if number > 0:
+                move_scales((number - 1) // 4, (number - 1) % 4)
         for t in range(PACK):
             nc.sync.dma_start(out=wo_sb[:, t, :], in_=wo_rows[t])
 
@@ -97,18 +120,11 @@ def tile_list_cauchy_point_occupancy_kernel(
         for quad in range(4):
             nc.scalar.dma_start(out=wcs_sb[32 * quad : 32 * quad + 4, :, :], in_=wc_scale_rows[4 * quad : 4 * quad + 4])
 
-        nc.vector.tensor_copy(out=sc_rows[:], in_=tab_sc[:].indirect(idx[:]))
-        for a in range(PASSES):
-            for quad in range(4):
-                row = 16 * a + 4 * quad
-                nc.scalar.dma_start(
-                    out=v_sc[a][32 * quad : 32 * quad + 4, :].bitcast(I32), in_=sc_rows[row : row + 4, :].bitcast(I32)
-                )
-
-        def quantise(src, width, name, tag=None):
-            codes = held([P, width], U32, name + "_q", tag=tag or name + "_q")
+        def quantise(src, width, name, codes=None):
+            if codes is None:
+                codes = held([P, width], U32, name + "_q")[:]
             scales = held([P, width], U8, name + "_s")
-            nc.vector.quantize_mx(out=codes[:].bitcast(E4M3), scales=scales[:], in_=src)
+            nc.vector.quantize_mx(out=codes.bitcast(E4M3), scales=scales[:], in_=src)
             return codes, scales
 
         def interleaved(ap):
@@ -120,46 +136,69 @@ def tile_list_cauchy_point_occupancy_kernel(
         def list_part(tile, lo, width):
             return tile[:, lo // 16 : (lo + width) // 16]
 
-        def gather_x(a, i, picked, lo, width):
+        def gather_x(a, i, lo, width):
             nc.vector.tensor_tensor(
-                picked[:, i, lo : lo + width],
+                xg[a][:, i, lo : lo + width],
                 x_sb[a][i][:].indirect(list_part(idx2, lo, width)),
                 wgt_sb[:, lo : lo + width],
                 ALU.mult,
             )
 
-        def round_x(picked, lo, width, name, tag=None):
+        def round_x(a, lo, width, name, codes=None):
             rounded = held([P, PACK * width], BF16, name + "_b")
-            nc.scalar.activation(interleaved(rounded[:]), planes(picked[:, :, lo : lo + width]), ACT.Copy, scale=-1.0)
-            return quantise(rounded[:], width, name, tag)
+            nc.scalar.activation(interleaved(rounded[:]), planes(xg[a][:, :, lo : lo + width]), ACT.Copy, scale=-1.0)
+            return quantise(rounded[:], width, name, codes)
 
-        def deal_wn(a, copy):
-            rounded = held([P, PACK * H], BF16, f"wnb{a}", tag="w_b")
+        def deal_wn(a):
+            rounded = held([P, PACK * H], BF16, f"wnb{a}")
             dst = rounded[:].rearrange("p (t s e i) -> p t s i e", t=PACK, e=RUN, i=PACK)
             src = wn_sb[a][:].rearrange("p i (s t e) -> p t s i e", t=PACK, e=RUN)
-            copy(out=dst, in_=src)
+            nc.scalar.copy(out=dst, in_=src)
             return quantise(rounded[:], H, f"wnq{a}")
 
-        d_ps = [[psum.tile([P, HALF], F32, name=f"d{b}{t}", tag=f"bank{b}{t}") for t in range(PACK)] for b in range(HALVES)]
+        d_ps = [[psum.tile([P, 2, CHUNK], F32, name=f"d{c}{u}", tag=f"bank{c}{u}") for u in range(2)] for c in range(CHUNKS)]
 
-        def neighbours_pass(a, b, wq, x_q, x_s, stop):
+        def neighbours_pass(a, c, wq, x_q, x_s):
             for t in range(PACK):
                 cols = slice(t * P, (t + 1) * P)
                 nc.tensor.matmul_mx(
-                    out=d_ps[b][t][:],
+                    out=d_ps[c][t // 2][:, t % 2, :],
                     lhsT=wq[0][:, cols].bitcast(E4M3),
                     lhsT_scale=wq[1][:, cols],
                     rhs=x_q.bitcast(E4M3),
                     rhs_scale=x_s,
-                    start=(a == 0),
-                    stop=stop,
+                    start=(a == 0 and t % 2 == 0),
+                    stop=False,
                 )
 
-        xg = [keep.tile([P, PACK, S], F32, name=f"xg{a}", tag="f32x4", bufs=2, align_bytes=64) for a in range(PASSES)]
+        def gather_words(a, c, v_q=None):
+            if v_q is None:
+                v_q = held([P, CHUNK], U32, f"vq{a}{c}")[:]
+            nc.vector.tensor_copy(out=v_q, in_=tab_sb[a][:].bitcast(U32).indirect(list_part(idx, c * CHUNK, CHUNK)))
+            return v_q
+
+        def centroids_pass(a, c, v_q, last):
+            for t in range(PACK):
+                for lo in range(0, CHUNK, FP4_N):
+                    nc.tensor.matmul_mx(
+                        out=d_ps[c][t // 2][:, t % 2, lo : lo + FP4_N],
+                        lhsT=wc_q[:, a, t * P // 2 : (t + 1) * P // 2].bitcast(U8).bitcast(E2M1),
+                        lhsT_scale=wc_s[:, a, t * P // 4 : (t + 1) * P // 4].bitcast(U8),
+                        rhs=v_q[:, lo : lo + FP4_N].bitcast(E4M3),
+                        rhs_scale=v_sc[a][:, c * CHUNK + lo : c * CHUNK + lo + FP4_N],
+                        start=False,
+                        stop=(last and t % 2 == 1 and lo + FP4_N == CHUNK),
+                    )
+
+        xg = [held([P, PACK, S], F32, f"xg{a}") for a in range(PASSES)]
         for i in range(PACK):
-            gather_x(0, i, xg[0], 0, S)
+            gather_x(0, i, 0, S)
+        gather_x(1, 0, 0, S)
+        x0 = [round_x(0, lo, 2 * CHUNK, f"xq0{lo}") for lo in range(0, S, 2 * CHUNK)]
+        gather_x(1, 1, 0, S)
+        gather_x(1, 2, 0, S)
         wc_q = held([P, PASSES, H // 2], I32, "wc_q")
-        wc_s = held([P, PASSES, H // 4], I32, "wc_s")
+        wc_s = held([P, PASSES, H // 4], I32, "wc_s", tag="x03")
         nc.vector.tensor_copy(
             out=wc_q[:].rearrange("p a (t s w) -> p a t s w", t=PACK, w=2),
             in_=wcw_sb[:].rearrange("p a (s t w) -> p a t s w", t=PACK, w=2),
@@ -168,107 +207,71 @@ def tile_list_cauchy_point_occupancy_kernel(
             out=wc_s[:].rearrange("p a (t s) -> p a t s", t=PACK),
             in_=wcs_sb[:].rearrange("p a (s t) -> p a t s", t=PACK),
         )
-
-        def gather_words(a, lo, width, name):
-            v_q = held([P, width], U32, name)
-            nc.vector.tensor_copy(out=v_q[:], in_=tab_sb[a][:].bitcast(U32).indirect(list_part(idx, lo, width)))
-            return v_q
-
-        def centroids_pass(a, b, v_q, stop):
-            for t in range(PACK):
-                nc.tensor.matmul_mx(
-                    out=d_ps[b][t][:],
-                    lhsT=wc_q[:, a, t * P // 2 : (t + 1) * P // 2].bitcast(U8).bitcast(E2M1),
-                    lhsT_scale=wc_s[:, a, t * P // 4 : (t + 1) * P // 4].bitcast(U8),
-                    rhs=v_q.bitcast(E4M3),
-                    rhs_scale=v_sc[a][:, b * HALF : (b + 1) * HALF],
-                    start=False,
-                    stop=stop,
-                )
-
-        halves = [slice(b * HALF, (b + 1) * HALF) for b in range(HALVES)]
-        gather_x(1, 0, xg[1], 0, S)
-        gather_x(1, 1, xg[1], 0, S)
-        x_q, x_s = round_x(xg[0], 0, S, "xq0")
-        wq0 = deal_wn(0, nc.scalar.copy)
-        v_q = gather_words(0, 0, S, "vq0")
-        for b in range(HALVES):
-            neighbours_pass(0, b, wq0, x_q[:, halves[b]], x_s[:, halves[b]], False)
-            centroids_pass(0, b, v_q[:, halves[b]], False)
-        gather_x(1, 2, xg[1], 0, S)
-        gather_x(1, 3, xg[1], 0, HALF)
-        gather_x(1, 3, xg[1], HALF, HALF)
-        wq1 = deal_wn(1, nc.vector.tensor_copy)
-        x_q, x_s = round_x(xg[1], 0, HALF, "xq10")
-        neighbours_pass(1, 0, wq1, x_q[:], x_s[:], False)
-        centroids_pass(1, 0, gather_words(1, 0, HALF, "vq10")[:], True)
-        centroids_pass(1, 1, gather_words(1, HALF, HALF, "vq11")[:], False)
-        x_q, x_s = round_x(xg[1], HALF, HALF, "xq11", "xq10_q")
-        neighbours_pass(1, 1, wq1, x_q[:], x_s[:], True)
         inv_gain = held([P, PACK], F32, "inv_gain", tag="x12")
         nc.vector.reciprocal(inv_gain[:], gain_sb[:, :, 0])
+        wq0 = deal_wn(0)
+        for c in range(CHUNKS):
+            x_q, x_s = x0[c // 2]
+            part = slice(c % 2 * CHUNK, (c % 2 + 1) * CHUNK)
+            neighbours_pass(0, c, wq0, x_q[:, part], x_s[:, part])
+        wq1 = deal_wn(1)
+        for c in range(CHUNKS):
+            gather_x(1, 3, c * CHUNK, CHUNK)
 
-        wo_b = held([P, PACK * N], BF16, "wo_b", tag="w_b")
+        late_v = late.tile([P, rest], U32, name="late_v", offset=0, align_bytes=64)
+        late_x = late.tile([P, rest], U32, name="late_x", offset=4 * rest, align_bytes=64)
+        for c in range(CHUNKS):
+            part = slice((c - 1) * CHUNK, c * CHUNK)
+            x_q, x_s = round_x(1, c * CHUNK, CHUNK, f"xq1{c}", late_x[:, part] if c else None)
+            neighbours_pass(1, c, wq1, x_q, x_s[:])
+            centroids_pass(0, c, gather_words(0, c, late_v[:, part] if c else None), False)
+            centroids_pass(1, c, gather_words(1, c), True)
+
+        wo_b = held([P, PACK * N], BF16, "wo_b", tag="wnb0")
         nc.vector.tensor_copy(out=interleaved(wo_b[:]), in_=planes(wo_sb[:]))
         wo_q, wo_s = quantise(wo_b[:], N, "woq")
 
         out_rows = out.rearrange("(m p) j -> p m j", p=P)
 
-        def square_vector(dst, src):
-            nc.vector.tensor_tensor(dst, src, src, ALU.mult)
-
-        def square_scalar(dst, src):
-            nc.scalar.activation(dst, src, ACT.Square)
-
-        vec, sca = nc.vector.tensor_copy, nc.scalar.copy
-        units = [
-            (0, 0, 256, square_vector, [(0, vec), (1, vec)]),
-            (0, 256, 256, square_vector, [(2, vec), (3, vec)]),
-            (1, 0, 256, square_vector, [(0, sca), (1, sca)]),
-            (1, 256, 128, square_vector, [(2, vec)]),
-            (1, 384, 128, square_scalar, [(3, sca)]),
-        ]
         roots = []
-        x_tags = [f"x{a}{i}" for a in range(PASSES) for i in range(PACK)]
-        for b, lo, width, square, banks in units:
-            if lo == 0:
-                d_sq = keep.tile([P, PACK, HALF], F32, name=f"dsq{b}", tag="f32x4", bufs=2, align_bytes=64)
-                for t in range(PACK):
-                    nc.scalar.activation(d_sq[:, t, :], d_ps[b][t][:], ACT.Square)
-            root = held([P, PACK, width], F32, f"root{b}{lo}", tag=x_tags[len(roots)])
+        for c in range(CHUNKS):
+            d_sq = held([P, PACK, CHUNK], F32, f"dsq{c}", tag=f"x0{c}")
+            for u in range(2):
+                nc.scalar.activation(d_sq[:, 2 * u : 2 * u + 2, :], d_ps[c][u][:], ACT.Square)
+            root = held([P, PACK, CHUNK], F32, f"root{c}", tag=["x10", "x11", "wn0", "wn1"][c])
             for t in range(PACK):
                 nc.scalar.activation(
                     root[:, t, :],
-                    d_sq[:, t, lo : lo + width],
+                    d_sq[:, t, :],
                     ACT.Abs_reciprocal_sqrt,
                     bias=inv_gain[:, t : t + 1],
                     scale=inv_gain[:, t : t + 1],
                 )
             roots.append(root)
 
+        copies = [nc.vector.tensor_copy, nc.scalar.copy]
         results = []
-        for root, (b, lo, width, square, banks) in zip(roots, units):
-            h_b = held([P, PACK * width], BF16, f"hb{b}{lo}")
-            square(interleaved(h_b[:]), planes(root[:]))
-            h_q, h_s = quantise(h_b[:], width, f"hq{b}{lo}")
-            per_bank = N // P // len(banks)
-            for place, (bank, copy) in enumerate(banks):
-                o_ps = psum.tile([P, per_bank, width], F32, name=f"o{b}{bank}", tag=f"bank{b}{bank}")
-                for u in range(per_bank):
-                    m = place * per_bank + u
+        for c, root in enumerate(roots):
+            h_b = held([P, PACK * CHUNK], BF16, f"hb{c}")
+            nc.vector.tensor_tensor(interleaved(h_b[:]), planes(root[:]), planes(root[:]), ALU.mult)
+            h_q, h_s = quantise(h_b[:], CHUNK, f"hq{c}")
+            for u in range(2):
+                o_ps = psum.tile([P, 2, CHUNK], F32, name=f"o{c}{u}", tag=f"bank{c}{u}")
+                for w in range(2):
+                    m = 2 * u + w
                     nc.tensor.matmul_mx(
-                        out=o_ps[:, u, :],
+                        out=o_ps[:, w, :],
                         lhsT=wo_q[:, m * P : (m + 1) * P].bitcast(E4M3),
                         lhsT_scale=wo_s[:, m * P : (m + 1) * P],
-                        rhs=h_q[:].bitcast(E4M3),
+                        rhs=h_q.bitcast(E4M3),
                         rhs_scale=h_s[:],
                         start=True,
                         stop=True,
                     )
-                rows = slice(place * per_bank, (place + 1) * per_bank)
-                results.append((o_ps, copy, out_rows[:, rows, b * HALF + lo : b * HALF + lo + width], [P, per_bank, width]))
+                copy = copies[0] if c == 0 or (c == CHUNKS - 1 and u == 0) else copies[1]
+                results.append((o_ps, copy, out_rows[:, 2 * u : 2 * u + 2, c * CHUNK : (c + 1) * CHUNK]))
 
-        for number, (o_ps, copy, dest, shape) in enumerate(results):
-            staged = held(shape, F32, f"staged{number}")
+        for number, (o_ps, copy, dest) in enumerate(results):
+            staged = held([P, 2, CHUNK], F32, f"staged{number}")
             copy(out=staged[:], in_=o_ps[:])
             nc.sync.dma_start(out=dest, in_=staged[:])

@@ -49,7 +49,7 @@ def tile_list_cauchy_point_occupancy_kernel(
         wcw_sb = held([P, PASSES, H // 2], I32, "wcw_sb")
         wcs_sb = held([P, PASSES, H // 4], I32, "wcs_sb")
         gain_sb = held([P, PACK, 8], F32, "gain_sb")
-        v_sc = [held([P, S], U8, f"v_sc{a}") for a in range(PASSES)]
+        v_sc = held([P, PASSES, S], U8, "v_sc")
         rest = S - CHUNK
         sc_rows = late.tile([P, S], U8, name="sc_rows", offset=4 * rest - S // 2, align_bytes=64)
 
@@ -66,15 +66,14 @@ def tile_list_cauchy_point_occupancy_kernel(
         nc.vector.memset(tab_sc[32:64, :].bitcast(I32), 0)
         nc.vector.memset(tab_sc[64:128, :].bitcast(I32), 0)
         nc.vector.memset(wcs_sb[:], 0)
-        for a in range(PASSES):
-            nc.vector.memset(v_sc[a][:].bitcast(I32), 0)
+        nc.vector.memset(v_sc[:].bitcast(I32), 0)
 
         warm = held([P, 2], F32, "warm")
         nc.vector.memset(warm[:, 0:1], 1.0)
         nc.scalar.activation(warm[:, 1:2], warm[:, 0:1], ACT.Abs_reciprocal_sqrt)
 
         nc.sync.dma_start(out=idx[:], in_=offs)
-        nc.sync.dma_start(out=tab_sc[0:32, :].bitcast(I32), in_=tab_scales.rearrange("a q t -> (a q) t").bitcast(I32))
+        nc.sync.dma_start(out=tab_sc[0:32, :].bitcast(I32), in_=tab_scales.bitcast(I32).rearrange("a q w -> q a w"))
         nc.sync.dma_start(out=idx2[:], in_=offs2)
         nc.sync.dma_start(out=wgt_sb[:], in_=wgt)
         for i in range(PACK):
@@ -82,10 +81,10 @@ def tile_list_cauchy_point_occupancy_kernel(
 
         nc.vector.tensor_copy(out=sc_rows[:], in_=tab_sc[:].indirect(idx[:]))
 
-        def move_scales(a, quad):
-            row = 16 * a + 4 * quad
-            nc.sync.dma_start(
-                out=v_sc[a][32 * quad : 32 * quad + 4, :].bitcast(I32), in_=sc_rows[row : row + 4, :].bitcast(I32)
+        def move_scales(queue, quad):
+            queue.dma_start(
+                out=v_sc[32 * quad : 32 * quad + 4, :, :].rearrange("p a s -> p (a s)").bitcast(I32),
+                in_=sc_rows[8 * quad : 8 * quad + 8, :].bitcast(I32),
             )
 
         def load_wn(a):
@@ -94,21 +93,16 @@ def tile_list_cauchy_point_occupancy_kernel(
         def load_wc():
             nc.sync.dma_start(out=wcw_sb[:], in_=wc_words.bitcast(I32).rearrange("a p w -> p a w"))
 
-        big_loads = [
-            lambda: load_x(1, 0),
-            lambda: load_x(1, 1),
-            lambda: load_x(1, 2),
-            load_wc,
-            lambda: load_wn(0),
-            lambda: load_wn(1),
-            lambda: load_x(1, 3),
-            lambda: load_tab(0),
-            lambda: load_tab(1),
-        ]
-        for number, load in enumerate(big_loads):
-            load()
-            if number > 0:
-                move_scales((number - 1) // 4, (number - 1) % 4)
+        load_x(1, 0)
+        load_x(1, 1)
+        load_x(1, 2)
+        load_wc()
+        load_wn(0)
+        load_wn(1)
+        load_x(1, 3)
+        load_tab(0)
+        load_tab(1)
+        move_scales(nc.sync, 3)
         for t in range(PACK):
             nc.sync.dma_start(out=wo_sb[:, t, :], in_=wo_rows[t])
 
@@ -118,7 +112,9 @@ def tile_list_cauchy_point_occupancy_kernel(
                 nc.gpsimd.dma_start(out=gain_sb[:, t, 0:1], in_=gain_cols[t])
         wc_scale_rows = wc_scales.bitcast(I32).rearrange("a q w -> q a w")
         for quad in range(4):
-            nc.scalar.dma_start(out=wcs_sb[32 * quad : 32 * quad + 4, :, :], in_=wc_scale_rows[4 * quad : 4 * quad + 4])
+            nc.gpsimd.dma_start(out=wcs_sb[32 * quad : 32 * quad + 4, :, :], in_=wc_scale_rows[4 * quad : 4 * quad + 4])
+        for quad in range(3):
+            move_scales(nc.gpsimd, quad)
 
         def quantise(src, width, name, codes=None):
             if codes is None:
@@ -185,7 +181,7 @@ def tile_list_cauchy_point_occupancy_kernel(
                         lhsT=wc_q[:, a, t * P // 2 : (t + 1) * P // 2].bitcast(U8).bitcast(E2M1),
                         lhsT_scale=wc_s[:, a, t * P // 4 : (t + 1) * P // 4].bitcast(U8),
                         rhs=v_q[:, lo : lo + FP4_N].bitcast(E4M3),
-                        rhs_scale=v_sc[a][:, c * CHUNK + lo : c * CHUNK + lo + FP4_N],
+                        rhs_scale=v_sc[:, a, c * CHUNK + lo : c * CHUNK + lo + FP4_N],
                         start=False,
                         stop=(last and t % 2 == 1 and lo + FP4_N == CHUNK),
                     )
@@ -198,7 +194,7 @@ def tile_list_cauchy_point_occupancy_kernel(
         gather_x(1, 1, 0, S)
         gather_x(1, 2, 0, S)
         wc_q = held([P, PASSES, H // 2], I32, "wc_q")
-        wc_s = held([P, PASSES, H // 4], I32, "wc_s", tag="x03")
+        wc_s = held([P, PASSES, H // 4], I32, "wc_s", tag="x11")
         nc.vector.tensor_copy(
             out=wc_q[:].rearrange("p a (t s w) -> p a t s w", t=PACK, w=2),
             in_=wcw_sb[:].rearrange("p a (s t w) -> p a t s w", t=PACK, w=2),
@@ -238,7 +234,7 @@ def tile_list_cauchy_point_occupancy_kernel(
             d_sq = held([P, PACK, CHUNK], F32, f"dsq{c}", tag=f"x0{c}")
             for u in range(2):
                 nc.scalar.activation(d_sq[:, 2 * u : 2 * u + 2, :], d_ps[c][u][:], ACT.Square)
-            root = held([P, PACK, CHUNK], F32, f"root{c}", tag=["x10", "x11", "wn0", "wn1"][c])
+            root = held([P, PACK, CHUNK], F32, f"root{c}", tag=["x10", "x13", "wn0", "wn1"][c])
             for t in range(PACK):
                 nc.scalar.activation(
                     root[:, t, :],

@@ -1,6 +1,7 @@
 from contextlib import ExitStack
 
 import concourse.mybir as mybir
+from concourse.masks import make_identity
 
 K, T, S, H, N = 1024, 2048, 1024, 512, 512
 FLOPS = 2 * S * (2 * K * H + H * N)
@@ -23,6 +24,9 @@ CHUNK = 256
 CHUNKS = S // CHUNK
 FP4_N = 128
 RUN = 4
+GROUPS = 8
+GROUP = P // GROUPS
+BLOCKS = S // P
 
 
 def tile_list_cauchy_point_occupancy_kernel(
@@ -63,6 +67,10 @@ def tile_list_cauchy_point_occupancy_kernel(
         def load_tab(a):
             nc.sync.dma_start(out=tab_sb[a][:], in_=tab_words[a].rearrange("p t i -> p (t i)").bitcast(I32))
 
+        wgt_rows = held([P, P], F32, "wgt_rows")
+        nc.vector.memset(wgt_rows[GROUPS * BLOCKS :, :], 0.0)
+        identity = held([P, P], F32, "identity")
+        make_identity(nc, identity[:])
         nc.vector.memset(tab_sc[32:64, :].bitcast(I32), 0)
         nc.vector.memset(tab_sc[64:128, :].bitcast(I32), 0)
         nc.vector.memset(wcs_sb[:], 0)
@@ -72,17 +80,31 @@ def tile_list_cauchy_point_occupancy_kernel(
         nc.vector.memset(warm[:, 0:1], 1.0)
         nc.scalar.activation(warm[:, 1:2], warm[:, 0:1], ACT.Abs_reciprocal_sqrt)
 
+        nc.sync.dma_start(
+            out=wgt_rows[: GROUPS * BLOCKS, :], in_=wgt.rearrange("(g e) (r c) -> e g r c", e=GROUP, c=P)[0]
+        )
         nc.sync.dma_start(out=idx[:], in_=offs)
         nc.sync.dma_start(out=tab_sc[0:32, :].bitcast(I32), in_=tab_scales.bitcast(I32).rearrange("a q w -> q a w"))
         nc.sync.dma_start(out=idx2[:], in_=offs2)
-        nc.sync.dma_start(out=wgt_sb[:], in_=wgt)
         for i in range(PACK):
             load_x(0, i)
 
+        turned = psum.tile([P, P], F32, name="turned", tag="bank00")
+        nc.tensor.transpose(turned[:], wgt_rows[:], identity[:])
+        by_block = turned[:, : GROUPS * BLOCKS].rearrange("c (g r) -> c r g", r=BLOCKS)
+        for half in range(2):
+            blocks = slice(half * BLOCKS // 2, (half + 1) * BLOCKS // 2)
+            spread = held([P, BLOCKS // 2, GROUPS, GROUP], F32, f"spread{half}")
+            nc.scalar.copy(out=spread[:], in_=by_block[:, blocks, :].unsqueeze(3).to_broadcast([P, BLOCKS // 2, GROUPS, GROUP]))
+            back = psum.tile([P, BLOCKS // 2, P], F32, name=f"back{half}", tag=f"bank1{half}")
+            for r in range(BLOCKS // 2):
+                nc.tensor.transpose(back[:, r, :], spread[:, r, :, :].rearrange("c g e -> c (g e)"), identity[:])
+            nc.scalar.copy(out=wgt_sb[:, half * S // 2 : (half + 1) * S // 2], in_=back[:].rearrange("p r c -> p (r c)"))
+
         nc.vector.tensor_copy(out=sc_rows[:], in_=tab_sc[:].indirect(idx[:]))
 
-        def move_scales(queue, quad):
-            queue.dma_start(
+        def move_scales(quad):
+            nc.sync.dma_start(
                 out=v_sc[32 * quad : 32 * quad + 4, :, :].rearrange("p a s -> p (a s)").bitcast(I32),
                 in_=sc_rows[8 * quad : 8 * quad + 8, :].bitcast(I32),
             )
@@ -93,16 +115,25 @@ def tile_list_cauchy_point_occupancy_kernel(
         def load_wc():
             nc.sync.dma_start(out=wcw_sb[:], in_=wc_words.bitcast(I32).rearrange("a p w -> p a w"))
 
-        load_x(1, 0)
-        load_x(1, 1)
-        load_x(1, 2)
+        wc_scale_rows = wc_scales.bitcast(I32).rearrange("a q w -> q a w")
+
+        def load_wc_scales(quad):
+            nc.sync.dma_start(out=wcs_sb[32 * quad : 32 * quad + 4, :, :], in_=wc_scale_rows[4 * quad : 4 * quad + 4])
+
+        for i in range(3):
+            load_x(1, i)
+            load_wc_scales(i)
         load_wc()
+        load_wc_scales(3)
         load_wn(0)
+        move_scales(0)
         load_wn(1)
+        move_scales(1)
         load_x(1, 3)
+        move_scales(2)
         load_tab(0)
         load_tab(1)
-        move_scales(nc.sync, 3)
+        move_scales(3)
         for t in range(PACK):
             nc.sync.dma_start(out=wo_sb[:, t, :], in_=wo_rows[t])
 
@@ -110,11 +141,6 @@ def tile_list_cauchy_point_occupancy_kernel(
         with nc.allow_non_contiguous_dma(reason="one gain value a partition"):
             for t in range(PACK):
                 nc.gpsimd.dma_start(out=gain_sb[:, t, 0:1], in_=gain_cols[t])
-        wc_scale_rows = wc_scales.bitcast(I32).rearrange("a q w -> q a w")
-        for quad in range(4):
-            nc.gpsimd.dma_start(out=wcs_sb[32 * quad : 32 * quad + 4, :, :], in_=wc_scale_rows[4 * quad : 4 * quad + 4])
-        for quad in range(3):
-            move_scales(nc.gpsimd, quad)
 
         def quantise(src, width, name, codes=None):
             if codes is None:
@@ -187,14 +213,16 @@ def tile_list_cauchy_point_occupancy_kernel(
                     )
 
         xg = [held([P, PACK, S], F32, f"xg{a}") for a in range(PASSES)]
-        for i in range(PACK):
+        gather_x(0, 0, 0, S // 2)
+        gather_x(0, 0, S // 2, S // 2)
+        for i in range(1, PACK):
             gather_x(0, i, 0, S)
         gather_x(1, 0, 0, S)
         x0 = [round_x(0, lo, 2 * CHUNK, f"xq0{lo}") for lo in range(0, S, 2 * CHUNK)]
         gather_x(1, 1, 0, S)
         gather_x(1, 2, 0, S)
         wc_q = held([P, PASSES, H // 2], I32, "wc_q")
-        wc_s = held([P, PASSES, H // 4], I32, "wc_s", tag="x11")
+        wc_s = held([P, PASSES, H // 4], I32, "wc_s")
         nc.vector.tensor_copy(
             out=wc_q[:].rearrange("p a (t s w) -> p a t s w", t=PACK, w=2),
             in_=wcw_sb[:].rearrange("p a (s t w) -> p a t s w", t=PACK, w=2),
@@ -224,8 +252,22 @@ def tile_list_cauchy_point_occupancy_kernel(
             centroids_pass(1, c, gather_words(1, c), True)
 
         wo_b = held([P, PACK * N], BF16, "wo_b", tag="wnb0")
-        nc.vector.tensor_copy(out=interleaved(wo_b[:]), in_=planes(wo_sb[:]))
-        wo_q, wo_s = quantise(wo_b[:], N, "woq")
+
+        def quantise_halves(src, width, name):
+            codes = held([P, width], U32, name + "_q")
+            scales = held([P, width], U8, name + "_s")
+            for lo in range(0, width, width // 2):
+                part = slice(lo, lo + width // 2)
+                nc.vector.quantize_mx(
+                    out=codes[:, part].bitcast(E4M3), scales=scales[:, part], in_=src[:, PACK * lo : PACK * (lo + width // 2)]
+                )
+            return codes[:], scales
+
+        for lo in range(0, N, N // 2):
+            nc.vector.tensor_copy(
+                out=interleaved(wo_b[:, PACK * lo : PACK * (lo + N // 2)]), in_=planes(wo_sb[:, :, lo : lo + N // 2])
+            )
+        wo_q, wo_s = quantise_halves(wo_b, N, "woq")
 
         out_rows = out.rearrange("(m p) j -> p m j", p=P)
 
@@ -249,8 +291,10 @@ def tile_list_cauchy_point_occupancy_kernel(
         results = []
         for c, root in enumerate(roots):
             h_b = held([P, PACK * CHUNK], BF16, f"hb{c}")
-            nc.vector.tensor_tensor(interleaved(h_b[:]), planes(root[:]), planes(root[:]), ALU.mult)
-            h_q, h_s = quantise(h_b[:], CHUNK, f"hq{c}")
+            for lo in range(0, CHUNK, CHUNK // 2):
+                src = planes(root[:, :, lo : lo + CHUNK // 2])
+                nc.vector.tensor_tensor(interleaved(h_b[:, PACK * lo : PACK * (lo + CHUNK // 2)]), src, src, ALU.mult)
+            h_q, h_s = quantise_halves(h_b, CHUNK, f"hq{c}")
             for u in range(2):
                 o_ps = psum.tile([P, 2, CHUNK], F32, name=f"o{c}{u}", tag=f"bank{c}{u}")
                 for w in range(2):

@@ -244,14 +244,13 @@ def tile_list_cauchy_point_occupancy_kernel(
 
         late_v = late.tile([P, rest], U32, name="late_v", offset=0, align_bytes=64)
         late_x = late.tile([P, rest], U32, name="late_x", offset=4 * rest, align_bytes=64)
-        for c in range(CHUNKS):
+
+        def first_stage(c, words):
             part = slice((c - 1) * CHUNK, c * CHUNK)
             x_q, x_s = round_x(1, c * CHUNK, CHUNK, f"xq1{c}", late_x[:, part] if c else None)
             neighbours_pass(1, c, wq1, x_q, x_s[:])
-            centroids_pass(0, c, gather_words(0, c, late_v[:, part] if c else None), False)
-            centroids_pass(1, c, gather_words(1, c), True)
-
-        wo_b = held([P, PACK * N], BF16, "wo_b", tag="wnb0")
+            for a in range(PASSES):
+                centroids_pass(a, c, gather_words(a, c, words[a]), a == PASSES - 1)
 
         def quantise_halves(src, width, name):
             codes = held([P, width], U32, name + "_q")
@@ -263,42 +262,41 @@ def tile_list_cauchy_point_occupancy_kernel(
                 )
             return codes[:], scales
 
-        for lo in range(0, N, N // 2):
-            nc.vector.tensor_copy(
-                out=interleaved(wo_b[:, PACK * lo : PACK * (lo + N // 2)]), in_=planes(wo_sb[:, :, lo : lo + N // 2])
-            )
-        wo_q, wo_s = quantise_halves(wo_b, N, "woq")
-
-        out_rows = out.rearrange("(m p) j -> p m j", p=P)
-
-        roots = []
-        for c in range(CHUNKS):
+        def squares(c):
             d_sq = held([P, PACK, CHUNK], F32, f"dsq{c}", tag=f"x0{c}")
             for u in range(2):
                 nc.scalar.activation(d_sq[:, 2 * u : 2 * u + 2, :], d_ps[c][u][:], ACT.Square)
-            root = held([P, PACK, CHUNK], F32, f"root{c}", tag=["x10", "x13", "wn0", "wn1"][c])
+            return d_sq
+
+        def inverse_roots(d_sq, lo, width, name, tag):
+            root = held([P, PACK, width], F32, name, tag=tag)
             for t in range(PACK):
                 nc.scalar.activation(
                     root[:, t, :],
-                    d_sq[:, t, :],
+                    d_sq[:, t, lo : lo + width],
                     ACT.Abs_reciprocal_sqrt,
                     bias=inv_gain[:, t : t + 1],
                     scale=inv_gain[:, t : t + 1],
                 )
-            roots.append(root)
+            return root
 
-        copies = [nc.vector.tensor_copy, nc.scalar.copy]
-        results = []
-        for c, root in enumerate(roots):
-            h_b = held([P, PACK * CHUNK], BF16, f"hb{c}")
-            for lo in range(0, CHUNK, CHUNK // 2):
-                src = planes(root[:, :, lo : lo + CHUNK // 2])
-                nc.vector.tensor_tensor(interleaved(h_b[:, PACK * lo : PACK * (lo + CHUNK // 2)]), src, src, ALU.mult)
-            h_q, h_s = quantise_halves(h_b, CHUNK, f"hq{c}")
-            for u in range(2):
-                o_ps = psum.tile([P, 2, CHUNK], F32, name=f"o{c}{u}", tag=f"bank{c}{u}")
-                for w in range(2):
-                    m = 2 * u + w
+        out_rows = out.rearrange("(m p) j -> p m j", p=P)
+
+        def second_stage(root, width, name, tags):
+            h_b = held([P, PACK * width], BF16, name + "_b")
+            for lo in range(0, width, P):
+                src = planes(root[:, :, lo : lo + P])
+                nc.vector.tensor_tensor(interleaved(h_b[:, PACK * lo : PACK * (lo + P)]), src, src, ALU.mult)
+            if width > P:
+                h_q, h_s = quantise_halves(h_b, width, name)
+            else:
+                h_q, h_s = quantise(h_b[:], width, name)
+            banks = []
+            per_bank = N // P // len(tags)
+            for u, tag in enumerate(tags):
+                o_ps = psum.tile([P, per_bank, width], F32, name=f"{name}_o{u}", tag=tag)
+                for w in range(per_bank):
+                    m = per_bank * u + w
                     nc.tensor.matmul_mx(
                         out=o_ps[:, w, :],
                         lhsT=wo_q[:, m * P : (m + 1) * P].bitcast(E4M3),
@@ -308,10 +306,40 @@ def tile_list_cauchy_point_occupancy_kernel(
                         start=True,
                         stop=True,
                     )
-                copy = copies[0] if c == 0 or (c == CHUNKS - 1 and u == 0) else copies[1]
-                results.append((o_ps, copy, out_rows[:, 2 * u : 2 * u + 2, c * CHUNK : (c + 1) * CHUNK]))
+                banks.append(o_ps)
+            return banks
 
-        for number, (o_ps, copy, dest) in enumerate(results):
-            staged = held([P, 2, CHUNK], F32, f"staged{number}")
-            copy(out=staged[:], in_=o_ps[:])
-            nc.sync.dma_start(out=dest, in_=staged[:])
+        def store(lo, width, banks, copies):
+            per_bank = N // P // len(banks)
+            for u, o_ps in enumerate(banks):
+                staged = held([P, per_bank, width], F32, f"staged{lo}{u}")
+                copies[u](out=staged[:], in_=o_ps[:])
+                nc.sync.dma_start(out=out_rows[:, per_bank * u : per_bank * (u + 1), lo : lo + width], in_=staged[:])
+
+        last = CHUNKS - 1
+        first_stage(0, [None, None])
+        for c in range(1, last):
+            first_stage(c, [late_v[:, (c - 1) * CHUNK : c * CHUNK], None])
+        roots = [inverse_roots(squares(c), 0, CHUNK, f"root{c}", ["x10", "x13", "wn0"][c]) for c in range(last)]
+
+        wo_b = held([P, PACK * N], BF16, "wo_b", tag="wnb0")
+        for lo in range(0, N, N // 2):
+            nc.vector.tensor_copy(
+                out=interleaved(wo_b[:, PACK * lo : PACK * (lo + N // 2)]), in_=planes(wo_sb[:, :, lo : lo + N // 2])
+            )
+        wo_q, wo_s = quantise_halves(wo_b, N, "woq")
+
+        by_scalar = [nc.scalar.copy, nc.scalar.copy]
+        banks = [second_stage(roots[0], CHUNK, "h0", ["bank00", "bank01"])]
+        last_v = held([P, PASSES, CHUNK], U32, "last_v", tag="x10")
+        first_stage(last, [last_v[:, a, :] for a in range(PASSES)])
+        last_sq = squares(last)
+        last_roots = [inverse_roots(last_sq, lo, P, f"root{last}{lo}", tag) for lo, tag in ((0, "wn1"), (P, "x11"))]
+        banks.extend(second_stage(roots[c], CHUNK, f"h{c}", [f"bank{c}0", f"bank{c}1"]) for c in range(1, last))
+        store(0, CHUNK, banks[0], by_scalar)
+        first_half = second_stage(last_roots[0], P, "h30", ["bank30"])
+        second_half = second_stage(last_roots[1], P, "h31", ["bank31", "bank00"])
+        for c in range(1, last):
+            store(c * CHUNK, CHUNK, banks[c], by_scalar)
+        store(last * CHUNK, P, first_half, [nc.vector.tensor_copy])
+        store(last * CHUNK + P, P, second_half, [nc.vector.tensor_copy, nc.scalar.copy])

@@ -80,13 +80,14 @@ def tile_list_cauchy_point_occupancy_kernel(
         nc.vector.memset(warm[:, 0:1], 1.0)
         nc.scalar.activation(warm[:, 1:2], warm[:, 0:1], ACT.Abs_reciprocal_sqrt)
 
-        nc.sync.dma_start(
+        nc.scalar.dma_start(out=tab_sc[0:32, :].bitcast(I32), in_=tab_scales.bitcast(I32).rearrange("a q w -> q a w"))
+        nc.scalar.dma_start(
             out=wgt_rows[: GROUPS * BLOCKS, :], in_=wgt.rearrange("(g e) (r c) -> e g r c", e=GROUP, c=P)[0]
         )
         nc.sync.dma_start(out=idx[:], in_=offs)
-        nc.sync.dma_start(out=tab_sc[0:32, :].bitcast(I32), in_=tab_scales.bitcast(I32).rearrange("a q w -> q a w"))
+        load_x(0, 0)
         nc.sync.dma_start(out=idx2[:], in_=offs2)
-        for i in range(PACK):
+        for i in range(1, PACK):
             load_x(0, i)
 
         turned = psum.tile([P, P], F32, name="turned", tag="bank00")
@@ -103,10 +104,10 @@ def tile_list_cauchy_point_occupancy_kernel(
 
         nc.vector.tensor_copy(out=sc_rows[:], in_=tab_sc[:].indirect(idx[:]))
 
-        def move_scales(quad):
+        def move_scales(quad, lo=0, hi=S):
             nc.sync.dma_start(
-                out=v_sc[32 * quad : 32 * quad + 4, :, :].rearrange("p a s -> p (a s)").bitcast(I32),
-                in_=sc_rows[8 * quad : 8 * quad + 8, :].bitcast(I32),
+                out=v_sc[32 * quad : 32 * quad + 4, :, lo:hi].bitcast(I32),
+                in_=sc_rows[8 * quad : 8 * quad + 8, lo:hi].bitcast(I32),
             )
 
         def load_wn(a):
@@ -125,15 +126,16 @@ def tile_list_cauchy_point_occupancy_kernel(
             load_wc_scales(i)
         load_wc()
         load_wc_scales(3)
-        load_wn(0)
         move_scales(0)
-        load_wn(1)
+        load_wn(0)
         move_scales(1)
-        load_x(1, 3)
+        load_wn(1)
         move_scales(2)
+        load_x(1, 3)
+        move_scales(3, 0, CHUNK)
         load_tab(0)
         load_tab(1)
-        move_scales(3)
+        move_scales(3, CHUNK, S)
         for t in range(PACK):
             nc.sync.dma_start(out=wo_sb[:, t, :], in_=wo_rows[t])
 
@@ -309,12 +311,11 @@ def tile_list_cauchy_point_occupancy_kernel(
                 banks.append(o_ps)
             return banks
 
-        def store(lo, width, banks, copies):
+        def store(lo, width, banks, u, copy):
             per_bank = N // P // len(banks)
-            for u, o_ps in enumerate(banks):
-                staged = held([P, per_bank, width], F32, f"staged{lo}{u}")
-                copies[u](out=staged[:], in_=o_ps[:])
-                nc.sync.dma_start(out=out_rows[:, per_bank * u : per_bank * (u + 1), lo : lo + width], in_=staged[:])
+            staged = held([P, per_bank, width], F32, f"staged{lo}{u}")
+            copy(out=staged[:], in_=banks[u][:])
+            nc.sync.dma_start(out=out_rows[:, per_bank * u : per_bank * (u + 1), lo : lo + width], in_=staged[:])
 
         last = CHUNKS - 1
         first_stage(0, [None, None])
@@ -329,17 +330,22 @@ def tile_list_cauchy_point_occupancy_kernel(
             )
         wo_q, wo_s = quantise_halves(wo_b, N, "woq")
 
-        by_scalar = [nc.scalar.copy, nc.scalar.copy]
+        vec, sca = nc.vector.tensor_copy, nc.scalar.copy
         banks = [second_stage(roots[0], CHUNK, "h0", ["bank00", "bank01"])]
+        for u in range(2):
+            store(0, CHUNK, banks[0], u, sca)
         last_v = held([P, PASSES, CHUNK], U32, "last_v", tag="x10")
         first_stage(last, [last_v[:, a, :] for a in range(PASSES)])
         last_sq = squares(last)
         last_roots = [inverse_roots(last_sq, lo, P, f"root{last}{lo}", tag) for lo, tag in ((0, "wn1"), (P, "x11"))]
-        banks.extend(second_stage(roots[c], CHUNK, f"h{c}", [f"bank{c}0", f"bank{c}1"]) for c in range(1, last))
-        store(0, CHUNK, banks[0], by_scalar)
+        banks.append(second_stage(roots[1], CHUNK, "h1", ["bank10", "bank11"]))
+        banks.append(second_stage(roots[2], CHUNK, "h2", ["bank20", "bank21"]))
+        store(CHUNK, CHUNK, banks[1], 0, vec)
         first_half = second_stage(last_roots[0], P, "h30", ["bank30"])
         second_half = second_stage(last_roots[1], P, "h31", ["bank31", "bank00"])
-        for c in range(1, last):
-            store(c * CHUNK, CHUNK, banks[c], by_scalar)
-        store(last * CHUNK, P, first_half, [nc.vector.tensor_copy])
-        store(last * CHUNK + P, P, second_half, [nc.vector.tensor_copy, nc.scalar.copy])
+        store(CHUNK, CHUNK, banks[1], 1, sca)
+        for u in range(2):
+            store(2 * CHUNK, CHUNK, banks[2], u, sca)
+        store(last * CHUNK, P, first_half, 0, sca)
+        store(last * CHUNK + P, P, second_half, 0, vec)
+        store(last * CHUNK + P, P, second_half, 1, sca)

@@ -51,9 +51,7 @@ def tile_list_cauchy_point_occupancy_kernel(
         wn_sb = [held([P, PACK, H], F32, f"wn{a}") for a in range(PASSES)]
         wo_sb = held([P, PACK, N], F32, "wo_sb")
         wcw_sb = held([P, PASSES, H // 2], I32, "wcw_sb")
-        wcs_sb = held([P, PASSES, H // 4], I32, "wcs_sb")
-        gain_sb = held([P, PACK, 8], F32, "gain_sb")
-        v_sc = held([P, PASSES, S], U8, "v_sc")
+        gain_row = held([1, H], F32, "gain_row")
         rest = S - CHUNK
         sc_rows = late.tile([P, S], U8, name="sc_rows", offset=4 * rest - S // 2, align_bytes=64)
 
@@ -67,18 +65,16 @@ def tile_list_cauchy_point_occupancy_kernel(
         def load_tab(a):
             nc.sync.dma_start(out=tab_sb[a][:], in_=tab_words[a].rearrange("p t i -> p (t i)").bitcast(I32))
 
+        warm = held([P, 2], F32, "warm")
+        nc.vector.memset(warm[:, 0:1], 1.0)
+        nc.scalar.activation(warm[:, 1:2], warm[:, 0:1], ACT.Abs_reciprocal_sqrt)
+
         wgt_rows = held([P, P], F32, "wgt_rows")
         nc.vector.memset(wgt_rows[GROUPS * BLOCKS :, :], 0.0)
         identity = held([P, P], F32, "identity")
         make_identity(nc, identity[:])
         nc.vector.memset(tab_sc[32:64, :].bitcast(I32), 0)
         nc.vector.memset(tab_sc[64:128, :].bitcast(I32), 0)
-        nc.vector.memset(wcs_sb[:], 0)
-        nc.vector.memset(v_sc[:].bitcast(I32), 0)
-
-        warm = held([P, 2], F32, "warm")
-        nc.vector.memset(warm[:, 0:1], 1.0)
-        nc.scalar.activation(warm[:, 1:2], warm[:, 0:1], ACT.Abs_reciprocal_sqrt)
 
         nc.scalar.dma_start(out=tab_sc[0:32, :].bitcast(I32), in_=tab_scales.bitcast(I32).rearrange("a q w -> q a w"))
         nc.scalar.dma_start(
@@ -89,6 +85,7 @@ def tile_list_cauchy_point_occupancy_kernel(
         nc.sync.dma_start(out=idx2[:], in_=offs2)
         for i in range(1, PACK):
             load_x(0, i)
+        nc.sync.dma_start(out=gain_row[:], in_=gain.rearrange("(o h) -> o h", o=1))
 
         turned = psum.tile([P, P], F32, name="turned", tag="bank00")
         nc.tensor.transpose(turned[:], wgt_rows[:], identity[:])
@@ -103,6 +100,13 @@ def tile_list_cauchy_point_occupancy_kernel(
             nc.scalar.copy(out=wgt_sb[:, half * S // 2 : (half + 1) * S // 2], in_=back[:].rearrange("p r c -> p (r c)"))
 
         nc.vector.tensor_copy(out=sc_rows[:], in_=tab_sc[:].indirect(idx[:]))
+
+        wcs_sb = held([P, PASSES, H // 4], I32, "wcs_sb", tag="spread0")
+        gain_dealt = held([P, PACK, P], F32, "gain_dealt", tag="spread1")
+        v_sc = held([P, PASSES, S], U8, "v_sc", tag="tab_sc")
+        nc.gpsimd.memset(wcs_sb[:], 0)
+        nc.gpsimd.memset(gain_dealt[:], 0.0)
+        nc.gpsimd.memset(v_sc[:].bitcast(I32), 0)
 
         def move_scales(quad, lo=0, hi=S):
             nc.sync.dma_start(
@@ -139,10 +143,13 @@ def tile_list_cauchy_point_occupancy_kernel(
         for t in range(PACK):
             nc.sync.dma_start(out=wo_sb[:, t, :], in_=wo_rows[t])
 
-        gain_cols = gain.rearrange("(s t e) -> t s e", t=PACK, e=RUN)
-        with nc.allow_non_contiguous_dma(reason="one gain value a partition"):
-            for t in range(PACK):
-                nc.gpsimd.dma_start(out=gain_sb[:, t, 0:1], in_=gain_cols[t])
+        nc.scalar.copy(
+            out=gain_dealt[0:1, :, :].rearrange("o t (s e) -> o t s e", e=RUN),
+            in_=gain_row[:].rearrange("o (s t e) -> o t s e", t=PACK, e=RUN),
+        )
+        gain_ps = psum.tile([P, PACK, P], F32, name="gain_ps", tag="bank31")
+        for t in range(PACK):
+            nc.tensor.transpose(gain_ps[:, t, :], gain_dealt[:, t, :], identity[:])
 
         def quantise(src, width, name, codes=None):
             if codes is None:
@@ -222,6 +229,8 @@ def tile_list_cauchy_point_occupancy_kernel(
         gather_x(1, 0, 0, S)
         x0 = [round_x(0, lo, 2 * CHUNK, f"xq0{lo}") for lo in range(0, S, 2 * CHUNK)]
         gather_x(1, 1, 0, S)
+        inv_gain = held([P, PACK], F32, "inv_gain", tag="x11")
+        nc.vector.reciprocal(inv_gain[:], gain_ps[:, :, 0])
         gather_x(1, 2, 0, S)
         wc_q = held([P, PASSES, H // 2], I32, "wc_q")
         wc_s = held([P, PASSES, H // 4], I32, "wc_s")
@@ -233,8 +242,6 @@ def tile_list_cauchy_point_occupancy_kernel(
             out=wc_s[:].rearrange("p a (t s) -> p a t s", t=PACK),
             in_=wcs_sb[:].rearrange("p a (s t) -> p a t s", t=PACK),
         )
-        inv_gain = held([P, PACK], F32, "inv_gain", tag="x12")
-        nc.vector.reciprocal(inv_gain[:], gain_sb[:, :, 0])
         wq0 = deal_wn(0)
         for c in range(CHUNKS):
             x_q, x_s = x0[c // 2]
@@ -265,7 +272,7 @@ def tile_list_cauchy_point_occupancy_kernel(
             return codes[:], scales
 
         def squares(c):
-            d_sq = held([P, PACK, CHUNK], F32, f"dsq{c}", tag=f"x0{c}")
+            d_sq = held([P, PACK, CHUNK], F32, f"dsq{c}", tag=["x00", "x01", "x02", "x03"][c])
             for u in range(2):
                 nc.scalar.activation(d_sq[:, 2 * u : 2 * u + 2, :], d_ps[c][u][:], ACT.Square)
             return d_sq
@@ -337,7 +344,7 @@ def tile_list_cauchy_point_occupancy_kernel(
         last_v = held([P, PASSES, CHUNK], U32, "last_v", tag="x10")
         first_stage(last, [last_v[:, a, :] for a in range(PASSES)])
         last_sq = squares(last)
-        last_roots = [inverse_roots(last_sq, lo, P, f"root{last}{lo}", tag) for lo, tag in ((0, "wn1"), (P, "x11"))]
+        last_roots = [inverse_roots(last_sq, lo, P, f"root{last}{lo}", tag) for lo, tag in ((0, "wn1"), (P, "x12"))]
         banks.append(second_stage(roots[1], CHUNK, "h1", ["bank10", "bank11"]))
         banks.append(second_stage(roots[2], CHUNK, "h2", ["bank20", "bank21"]))
         store(CHUNK, CHUNK, banks[1], 0, vec)

@@ -83,26 +83,28 @@ def tile_list_cauchy_point_occupancy_kernel(
         nc.sync.dma_start(out=idx[:], in_=offs)
         load_x(0, 0)
         nc.sync.dma_start(out=idx2[:], in_=offs2)
-        for i in range(1, PACK):
-            load_x(0, i)
+        load_x(0, 1)
         nc.sync.dma_start(out=gain_row[:], in_=gain.rearrange("(o h) -> o h", o=1))
+        for i in range(2, PACK):
+            load_x(0, i)
 
         turned = psum.tile([P, P], F32, name="turned", tag="bank00")
         nc.tensor.transpose(turned[:], wgt_rows[:], identity[:])
         by_block = turned[:, : GROUPS * BLOCKS].rearrange("c (g r) -> c r g", r=BLOCKS)
-        for half in range(2):
-            blocks = slice(half * BLOCKS // 2, (half + 1) * BLOCKS // 2)
-            spread = held([P, BLOCKS // 2, GROUPS, GROUP], F32, f"spread{half}")
-            nc.scalar.copy(out=spread[:], in_=by_block[:, blocks, :].unsqueeze(3).to_broadcast([P, BLOCKS // 2, GROUPS, GROUP]))
-            back = psum.tile([P, BLOCKS // 2, P], F32, name=f"back{half}", tag=f"bank1{half}")
-            for r in range(BLOCKS // 2):
+        spread_runs = [(0, 2), (2, 4), (4, 8)]
+        for number, (lo, hi) in enumerate(spread_runs):
+            shape = [P, hi - lo, GROUPS, GROUP]
+            spread = held(shape, F32, f"spread{number}")
+            nc.scalar.copy(out=spread[:], in_=by_block[:, lo:hi, :].unsqueeze(3).to_broadcast(shape))
+            back = psum.tile([P, hi - lo, P], F32, name=f"back{number}", tag=f"bank{number + 1}0")
+            for r in range(hi - lo):
                 nc.tensor.transpose(back[:, r, :], spread[:, r, :, :].rearrange("c g e -> c (g e)"), identity[:])
-            nc.scalar.copy(out=wgt_sb[:, half * S // 2 : (half + 1) * S // 2], in_=back[:].rearrange("p r c -> p (r c)"))
+            nc.scalar.copy(out=wgt_sb[:, lo * P : hi * P], in_=back[:].rearrange("p r c -> p (r c)"))
 
         nc.vector.tensor_copy(out=sc_rows[:], in_=tab_sc[:].indirect(idx[:]))
 
         wcs_sb = held([P, PASSES, H // 4], I32, "wcs_sb", tag="spread0")
-        gain_dealt = held([P, PACK, P], F32, "gain_dealt", tag="spread1")
+        gain_dealt = held([P, PACK, P], F32, "gain_dealt", tag="spread2")
         v_sc = held([P, PASSES, S], U8, "v_sc", tag="tab_sc")
         nc.gpsimd.memset(wcs_sb[:], 0)
         nc.gpsimd.memset(gain_dealt[:], 0.0)
@@ -128,14 +130,14 @@ def tile_list_cauchy_point_occupancy_kernel(
         for i in range(3):
             load_x(1, i)
             load_wc_scales(i)
-        load_wc()
+        load_wn(1)
         load_wc_scales(3)
         move_scales(0)
         load_wn(0)
         move_scales(1)
-        load_wn(1)
-        move_scales(2)
         load_x(1, 3)
+        load_wc()
+        move_scales(2)
         move_scales(3, 0, CHUNK)
         load_tab(0)
         load_tab(1)
@@ -222,8 +224,8 @@ def tile_list_cauchy_point_occupancy_kernel(
                     )
 
         xg = [held([P, PACK, S], F32, f"xg{a}") for a in range(PASSES)]
-        gather_x(0, 0, 0, S // 2)
-        gather_x(0, 0, S // 2, S // 2)
+        for lo, hi in spread_runs:
+            gather_x(0, 0, lo * P, (hi - lo) * P)
         for i in range(1, PACK):
             gather_x(0, i, 0, S)
         gather_x(1, 0, 0, S)
@@ -235,21 +237,21 @@ def tile_list_cauchy_point_occupancy_kernel(
         wc_q = held([P, PASSES, H // 2], I32, "wc_q")
         wc_s = held([P, PASSES, H // 4], I32, "wc_s")
         nc.vector.tensor_copy(
-            out=wc_q[:].rearrange("p a (t s w) -> p a t s w", t=PACK, w=2),
-            in_=wcw_sb[:].rearrange("p a (s t w) -> p a t s w", t=PACK, w=2),
-        )
-        nc.vector.tensor_copy(
             out=wc_s[:].rearrange("p a (t s) -> p a t s", t=PACK),
             in_=wcs_sb[:].rearrange("p a (s t) -> p a t s", t=PACK),
         )
+        wq1 = deal_wn(1)
         wq0 = deal_wn(0)
         for c in range(CHUNKS):
             x_q, x_s = x0[c // 2]
             part = slice(c % 2 * CHUNK, (c % 2 + 1) * CHUNK)
             neighbours_pass(0, c, wq0, x_q[:, part], x_s[:, part])
-        wq1 = deal_wn(1)
         for c in range(CHUNKS):
             gather_x(1, 3, c * CHUNK, CHUNK)
+        nc.vector.tensor_copy(
+            out=wc_q[:].rearrange("p a (t s w) -> p a t s w", t=PACK, w=2),
+            in_=wcw_sb[:].rearrange("p a (s t w) -> p a t s w", t=PACK, w=2),
+        )
 
         late_v = late.tile([P, rest], U32, name="late_v", offset=0, align_bytes=64)
         late_x = late.tile([P, rest], U32, name="late_x", offset=4 * rest, align_bytes=64)

@@ -161,10 +161,10 @@ def tile_list_cauchy_point_occupancy_kernel(
             return codes, scales
 
         def interleaved(ap):
-            return ap.rearrange("p (c i t) -> p c t i", i=2, t=PACK)
+            return ap.rearrange("p (c i t) -> p c t i", i=4, t=PACK)
 
         def planes(ap):
-            return ap.rearrange("p t (c i) -> p c t i", i=2)
+            return ap.rearrange("p t (c i) -> p c t i", i=4)
 
         def list_part(tile, lo, width):
             return tile[:, lo // 16 : (lo + width) // 16]
@@ -258,7 +258,7 @@ def tile_list_cauchy_point_occupancy_kernel(
 
         def first_stage(c, words):
             part = slice((c - 1) * CHUNK, c * CHUNK)
-            x_q, x_s = round_x(1, c * CHUNK, CHUNK, f"xq1{c}", late_x[:, part] if c else None)
+            x_q, x_s = round_x(1, c * CHUNK, CHUNK, f"xq1{c}", late_x[:, part] if c > 1 else None)
             neighbours_pass(1, c, wq1, x_q, x_s[:])
             for a in range(PASSES):
                 centroids_pass(a, c, gather_words(a, c, words[a]), a == PASSES - 1)

@@ -22,7 +22,6 @@ PACK = 4
 PASSES = K // (P * PACK)
 CHUNK = 256
 CHUNKS = S // CHUNK
-FP4_N = 128
 RUN = 4
 GROUPS = 8
 GROUP = P // GROUPS
@@ -130,10 +129,10 @@ def tile_list_cauchy_point_occupancy_kernel(
         for i in range(3):
             load_x(1, i)
             load_wc_scales(i)
-        load_wn(1)
+        load_wn(0)
         load_wc_scales(3)
         move_scales(0)
-        load_wn(0)
+        load_wn(1)
         move_scales(1)
         load_x(1, 3)
         load_wc()
@@ -212,16 +211,15 @@ def tile_list_cauchy_point_occupancy_kernel(
 
         def centroids_pass(a, c, v_q, last):
             for t in range(PACK):
-                for lo in range(0, CHUNK, FP4_N):
-                    nc.tensor.matmul_mx(
-                        out=d_ps[c][t // 2][:, t % 2, lo : lo + FP4_N],
-                        lhsT=wc_q[:, a, t * P // 2 : (t + 1) * P // 2].bitcast(U8).bitcast(E2M1),
-                        lhsT_scale=wc_s[:, a, t * P // 4 : (t + 1) * P // 4].bitcast(U8),
-                        rhs=v_q[:, lo : lo + FP4_N].bitcast(E4M3),
-                        rhs_scale=v_sc[:, a, c * CHUNK + lo : c * CHUNK + lo + FP4_N],
-                        start=False,
-                        stop=(last and t % 2 == 1 and lo + FP4_N == CHUNK),
-                    )
+                nc.tensor.matmul_mx(
+                    out=d_ps[c][t // 2][:, t % 2, :],
+                    lhsT=wc_q[:, a, t * P // 2 : (t + 1) * P // 2].bitcast(U8).bitcast(E2M1),
+                    lhsT_scale=wc_s[:, a, t * P // 4 : (t + 1) * P // 4].bitcast(U8),
+                    rhs=v_q.bitcast(E4M3),
+                    rhs_scale=v_sc[:, a, c * CHUNK : (c + 1) * CHUNK],
+                    start=False,
+                    stop=(last and t % 2 == 1),
+                )
 
         xg = [held([P, PACK, S], F32, f"xg{a}") for a in range(PASSES)]
         for lo, hi in spread_runs:
@@ -240,14 +238,15 @@ def tile_list_cauchy_point_occupancy_kernel(
             out=wc_s[:].rearrange("p a (t s) -> p a t s", t=PACK),
             in_=wcs_sb[:].rearrange("p a (s t) -> p a t s", t=PACK),
         )
-        wq1 = deal_wn(1)
         wq0 = deal_wn(0)
         for c in range(CHUNKS):
             x_q, x_s = x0[c // 2]
             part = slice(c % 2 * CHUNK, (c % 2 + 1) * CHUNK)
             neighbours_pass(0, c, wq0, x_q[:, part], x_s[:, part])
-        for c in range(CHUNKS):
+        for c in range(2):
             gather_x(1, 3, c * CHUNK, CHUNK)
+        wq1 = deal_wn(1)
+        gather_x(1, 3, S // 2, S // 2)
         nc.vector.tensor_copy(
             out=wc_q[:].rearrange("p a (t s w) -> p a t s w", t=PACK, w=2),
             in_=wcw_sb[:].rearrange("p a (s t w) -> p a t s w", t=PACK, w=2),

@@ -354,6 +354,8 @@ def tile_list_cauchy_point_occupancy_kernel(
         store(CHUNK, CHUNK, banks[1], 1, sca)
         for u in range(2):
             store(2 * CHUNK, CHUNK, banks[2], u, sca)
-        store(last * CHUNK, P, first_half, 0, sca)
-        store(last * CHUNK + P, P, second_half, 0, vec)
-        store(last * CHUNK + P, P, second_half, 1, sca)
+        staged = held([P, N // P, CHUNK], F32, "staged_last")
+        sca(out=staged[:, :, :P], in_=first_half[0][:])
+        for u, copy in enumerate((vec, sca)):
+            copy(out=staged[:, 2 * u : 2 * u + 2, P:], in_=second_half[u][:])
+            nc.sync.dma_start(out=out_rows[:, 2 * u : 2 * u + 2, last * CHUNK :], in_=staged[:, 2 * u : 2 * u + 2, :])

@@ -349,13 +349,13 @@ def tile_list_cauchy_point_occupancy_kernel(
         banks.append(second_stage(roots[1], CHUNK, "h1", ["bank10", "bank11"]))
         banks.append(second_stage(roots[2], CHUNK, "h2", ["bank20", "bank21"]))
         store(CHUNK, CHUNK, banks[1], 0, vec)
-        first_half = second_stage(last_roots[0], P, "h30", ["bank30"])
+        first_half = second_stage(last_roots[0], P, "h30", ["bank30", "bank01"])
         second_half = second_stage(last_roots[1], P, "h31", ["bank31", "bank00"])
         store(CHUNK, CHUNK, banks[1], 1, sca)
         for u in range(2):
             store(2 * CHUNK, CHUNK, banks[2], u, sca)
         staged = held([P, N // P, CHUNK], F32, "staged_last")
-        sca(out=staged[:, :, :P], in_=first_half[0][:])
         for u, copy in enumerate((vec, sca)):
+            copy(out=staged[:, 2 * u : 2 * u + 2, :P], in_=first_half[u][:])
             copy(out=staged[:, 2 * u : 2 * u + 2, P:], in_=second_half[u][:])
             nc.sync.dma_start(out=out_rows[:, 2 * u : 2 * u + 2, last * CHUNK :], in_=staged[:, 2 * u : 2 * u + 2, :])

from contextlib import ExitStack

import concourse.mybir as mybir
from concourse.masks import make_identity

K, T, S, H, N = 1024, 2048, 1024, 512, 512
FLOPS = 2 * S * (2 * K * H + H * N)

F32 = mybir.dt.float32
BF16 = mybir.dt.bfloat16
I32 = mybir.dt.int32
U32 = mybir.dt.uint32
U16 = mybir.dt.uint16
U8 = mybir.dt.uint8
E4M3 = mybir.dt.float8_e4m3fn_x4
E2M1 = mybir.dt.float4_e2m1fn_x4
ACT = mybir.ActivationFunctionType
ALU = mybir.AluOpType

P = 128
PACK = 4
PASSES = K // (P * PACK)
CHUNK = 256
CHUNKS = S // CHUNK
RUN = 4
GROUPS = 8
GROUP = P // GROUPS
BLOCKS = S // P


def tile_list_cauchy_point_occupancy_kernel(
    tc, xT, wgt, offs2, tab_words, tab_scales, offs, wn, wc_words, wc_scales, gain, wo, out
):
    nc = tc.nc
    with ExitStack() as ctx:
        lists = ctx.enter_context(tc.tile_pool(name="lists", bufs=1))
        keep = ctx.enter_context(tc.tile_pool(name="keep", bufs=1))
        late = ctx.enter_context(tc.tile_pool(name="late", bufs=1))
        psum = ctx.enter_context(tc.psum_pool(name="psum", bufs=1))

        def held(shape, dtype, name, tag=None):
            return keep.tile(shape, dtype, name=name, tag=tag or name, align_bytes=64)

        idx = lists.tile([P, S // 16], U16, name="idx")
        idx2 = lists.tile([P, S // 16], U16, name="idx2")
        tab_sc = held([P, T], U8, "tab_sc")
        wgt_sb = held([P, S], F32, "wgt_sb")
        x_sb = [[held([P, T], F32, f"x{a}{i}") for i in range(PACK)] for a in range(PASSES)]
        tab_sb = [held([P, T], I32, f"tab{a}") for a in range(PASSES)]
        wn_sb = [held([P, PACK, H], F32, f"wn{a}") for a in range(PASSES)]
        wo_sb = held([P, PACK, N], F32, "wo_sb")
        wcw_sb = held([P, PASSES, H // 2], I32, "wcw_sb")
        gain_row = held([1, H], F32, "gain_row")
        rest = S - CHUNK
        sc_rows = late.tile([P, S], U8, name="sc_rows", offset=4 * rest - S // 2, align_bytes=64)

        x_rows = xT.rearrange("(a p i) t -> a i p t", a=PASSES, i=PACK)
        wn_rows = wn.rearrange("(a p i) h -> a p i h", a=PASSES, i=PACK)
        wo_rows = wo.rearrange("(s t e) n -> t s e n", t=PACK, e=RUN)

        def load_x(a, i):
            nc.sync.dma_start(out=x_sb[a][i][:], in_=x_rows[a, i])

        def load_tab(a):
            nc.sync.dma_start(out=tab_sb[a][:], in_=tab_words[a].rearrange("p t i -> p (t i)").bitcast(I32))

        warm = held([P, 2], F32, "warm")
        nc.vector.memset(warm[:, 0:1], 1.0)
        nc.scalar.activation(warm[:, 1:2], warm[:, 0:1], ACT.Abs_reciprocal_sqrt)

        wgt_rows = held([P, P], F32, "wgt_rows")
        nc.vector.memset(wgt_rows[GROUPS * BLOCKS :, :], 0.0)
        identity = held([P, P], F32, "identity")
        make_identity(nc, identity[:])
        nc.vector.memset(tab_sc[32:64, :].bitcast(I32), 0)
        nc.vector.memset(tab_sc[64:128, :].bitcast(I32), 0)

        nc.scalar.dma_start(out=tab_sc[0:32, :].bitcast(I32), in_=tab_scales.bitcast(I32).rearrange("a q w -> q a w"))
        nc.scalar.dma_start(
            out=wgt_rows[: GROUPS * BLOCKS, :], in_=wgt.rearrange("(g e) (r c) -> e g r c", e=GROUP, c=P)[0]
        )
        nc.sync.dma_start(out=idx[:], in_=offs)
        load_x(0, 0)
        nc.sync.dma_start(out=idx2[:], in_=offs2)
        load_x(0, 1)
        nc.sync.dma_start(out=gain_row[:], in_=gain.rearrange("(o h) -> o h", o=1))
        for i in range(2, PACK):
            load_x(0, i)

        turned = psum.tile([P, P], F32, name="turned", tag="bank00")
        nc.tensor.transpose(turned[:], wgt_rows[:], identity[:])
        by_block = turned[:, : GROUPS * BLOCKS].rearrange("c (g r) -> c r g", r=BLOCKS)
        spread_runs = [(0, 2), (2, 4), (4, 8)]
        for number, (lo, hi) in enumerate(spread_runs):
            shape = [P, hi - lo, GROUPS, GROUP]
            spread = held(shape, F32, f"spread{number}")
            nc.scalar.copy(out=spread[:], in_=by_block[:, lo:hi, :].unsqueeze(3).to_broadcast(shape))
            back = psum.tile([P, hi - lo, P], F32, name=f"back{number}", tag=f"bank{number + 1}0")
            for r in range(hi - lo):
                nc.tensor.transpose(back[:, r, :], spread[:, r, :, :].rearrange("c g e -> c (g e)"), identity[:])
            nc.scalar.copy(out=wgt_sb[:, lo * P : hi * P], in_=back[:].rearrange("p r c -> p (r c)"))

        nc.vector.tensor_copy(out=sc_rows[:], in_=tab_sc[:].indirect(idx[:]))

        wcs_sb = held([P, PASSES, H // 4], I32, "wcs_sb", tag="spread0")
        gain_dealt = held([P, PACK, P], F32, "gain_dealt", tag="spread2")
        v_sc = held([P, PASSES, S], U8, "v_sc", tag="tab_sc")
        nc.gpsimd.memset(wcs_sb[:], 0)
        nc.gpsimd.memset(gain_dealt[:], 0.0)
        nc.gpsimd.memset(v_sc[:].bitcast(I32), 0)

        def move_scales(quad, lo=0, hi=S):
            nc.sync.dma_start(
                out=v_sc[32 * quad : 32 * quad + 4, :, lo:hi].bitcast(I32),
                in_=sc_rows[8 * quad : 8 * quad + 8, lo:hi].bitcast(I32),
            )

        def load_wn(a):
            nc.sync.dma_start(out=wn_sb[a][:], in_=wn_rows[a])

        def load_wc():
            nc.sync.dma_start(out=wcw_sb[:], in_=wc_words.bitcast(I32).rearrange("a p w -> p a w"))

        wc_scale_rows = wc_scales.bitcast(I32).rearrange("a q w -> q a w")

        def load_wc_scales(quad):
            nc.sync.dma_start(out=wcs_sb[32 * quad : 32 * quad + 4, :, :], in_=wc_scale_rows[4 * quad : 4 * quad + 4])

        for i in range(3):
            load_x(1, i)
            load_wc_scales(i)
        load_wn(0)
        load_wc_scales(3)
        move_scales(0)
        load_wn(1)
        move_scales(1)
        load_x(1, 3)
        load_wc()
        move_scales(2)
        move_scales(3, 0, CHUNK)
        load_tab(0)
        load_tab(1)
        move_scales(3, CHUNK, S)
        for t in range(PACK):
            nc.sync.dma_start(out=wo_sb[:, t, :], in_=wo_rows[t])

        nc.scalar.copy(
            out=gain_dealt[0:1, :, :].rearrange("o t (s e) -> o t s e", e=RUN),
            in_=gain_row[:].rearrange("o (s t e) -> o t s e", t=PACK, e=RUN),
        )
        gain_ps = psum.tile([P, PACK, P], F32, name="gain_ps", tag="bank31")
        for t in range(PACK):
            nc.tensor.transpose(gain_ps[:, t, :], gain_dealt[:, t, :], identity[:])

        def quantise(src, width, name, codes=None):
            if codes is None:
                codes = held([P, width], U32, name + "_q")[:]
            scales = held([P, width], U8, name + "_s")
            nc.vector.quantize_mx(out=codes.bitcast(E4M3), scales=scales[:], in_=src)
            return codes, scales

        def interleaved(ap):
            return ap.rearrange("p (c i t) -> p c t i", i=4, t=PACK)

        def planes(ap):
            return ap.rearrange("p t (c i) -> p c t i", i=4)

        def list_part(tile, lo, width):
            return tile[:, lo // 16 : (lo + width) // 16]

        def gather_x(a, i, lo, width):
            nc.vector.tensor_tensor(
                xg[a][:, i, lo : lo + width],
                x_sb[a][i][:].indirect(list_part(idx2, lo, width)),
                wgt_sb[:, lo : lo + width],
                ALU.mult,
            )

        def round_x(a, lo, width, name, codes=None):
            rounded = held([P, PACK * width], BF16, name + "_b")
            nc.scalar.activation(interleaved(rounded[:]), planes(xg[a][:, :, lo : lo + width]), ACT.Copy, scale=-1.0)
            return quantise(rounded[:], width, name, codes)

        def deal_wn(a):
            rounded = held([P, PACK * H], BF16, f"wnb{a}")
            dst = rounded[:].rearrange("p (t s e i) -> p t s i e", t=PACK, e=RUN, i=PACK)
            src = wn_sb[a][:].rearrange("p i (s t e) -> p t s i e", t=PACK, e=RUN)
            nc.scalar.copy(out=dst, in_=src)
            return quantise(rounded[:], H, f"wnq{a}")

        d_ps = [[psum.tile([P, 2, CHUNK], F32, name=f"d{c}{u}", tag=f"bank{c}{u}") for u in range(2)] for c in range(CHUNKS)]

        def neighbours_pass(a, c, wq, x_q, x_s):
            for t in range(PACK):
                cols = slice(t * P, (t + 1) * P)
                nc.tensor.matmul_mx(
                    out=d_ps[c][t // 2][:, t % 2, :],
                    lhsT=wq[0][:, cols].bitcast(E4M3),
                    lhsT_scale=wq[1][:, cols],
                    rhs=x_q.bitcast(E4M3),
                    rhs_scale=x_s,
                    start=(a == 0 and t % 2 == 0),
                    stop=False,
                )

        def gather_words(a, c, v_q=None):
            if v_q is None:
                v_q = held([P, CHUNK], U32, f"vq{a}{c}")[:]
            nc.vector.tensor_copy(out=v_q, in_=tab_sb[a][:].bitcast(U32).indirect(list_part(idx, c * CHUNK, CHUNK)))
            return v_q

        def centroids_pass(a, c, v_q, last):
            for t in range(PACK):
                nc.tensor.matmul_mx(
                    out=d_ps[c][t // 2][:, t % 2, :],
                    lhsT=wc_q[:, a, t * P // 2 : (t + 1) * P // 2].bitcast(U8).bitcast(E2M1),
                    lhsT_scale=wc_s[:, a, t * P // 4 : (t + 1) * P // 4].bitcast(U8),
                    rhs=v_q.bitcast(E4M3),
                    rhs_scale=v_sc[:, a, c * CHUNK : (c + 1) * CHUNK],
                    start=False,
                    stop=(last and t % 2 == 1),
                )

        xg = [held([P, PACK, S], F32, f"xg{a}") for a in range(PASSES)]
        for lo, hi in spread_runs:
            gather_x(0, 0, lo * P, (hi - lo) * P)
        for i in range(1, PACK):
            gather_x(0, i, 0, S)
        gather_x(1, 0, 0, S)
        x0 = [round_x(0, lo, 2 * CHUNK, f"xq0{lo}") for lo in range(0, S, 2 * CHUNK)]
        gather_x(1, 1, 0, S)
        inv_gain = held([P, PACK], F32, "inv_gain", tag="x11")
        nc.vector.reciprocal(inv_gain[:], gain_ps[:, :, 0])
        gather_x(1, 2, 0, S)
        wc_q = held([P, PASSES, H // 2], I32, "wc_q")
        wc_s = held([P, PASSES, H // 4], I32, "wc_s")
        nc.vector.tensor_copy(
            out=wc_s[:].rearrange("p a (t s) -> p a t s", t=PACK),
            in_=wcs_sb[:].rearrange("p a (s t) -> p a t s", t=PACK),
        )
        wq0 = deal_wn(0)
        for c in range(CHUNKS):
            x_q, x_s = x0[c // 2]
            part = slice(c % 2 * CHUNK, (c % 2 + 1) * CHUNK)
            neighbours_pass(0, c, wq0, x_q[:, part], x_s[:, part])
        for c in range(2):
            gather_x(1, 3, c * CHUNK, CHUNK)
        wq1 = deal_wn(1)
        gather_x(1, 3, S // 2, S // 2)
        nc.vector.tensor_copy(
            out=wc_q[:].rearrange("p a (t s w) -> p a t s w", t=PACK, w=2),
            in_=wcw_sb[:].rearrange("p a (s t w) -> p a t s w", t=PACK, w=2),
        )

        late_v = late.tile([P, rest], U32, name="late_v", offset=0, align_bytes=64)
        late_x = late.tile([P, rest], U32, name="late_x", offset=4 * rest, align_bytes=64)

        def first_stage(c, words):
            part = slice((c - 1) * CHUNK, c * CHUNK)
            x_q, x_s = round_x(1, c * CHUNK, CHUNK, f"xq1{c}", late_x[:, part] if c > 1 else None)
            neighbours_pass(1, c, wq1, x_q, x_s[:])
            for a in range(PASSES):
                centroids_pass(a, c, gather_words(a, c, words[a]), a == PASSES - 1)

        def quantise_halves(src, width, name):
            codes = held([P, width], U32, name + "_q")
            scales = held([P, width], U8, name + "_s")
            for lo in range(0, width, width // 2):
                part = slice(lo, lo + width // 2)
                nc.vector.quantize_mx(
                    out=codes[:, part].bitcast(E4M3), scales=scales[:, part], in_=src[:, PACK * lo : PACK * (lo + width // 2)]
                )
            return codes[:], scales

        def squares(c):
            d_sq = held([P, PACK, CHUNK], F32, f"dsq{c}", tag=["x00", "x01", "x02", "x03"][c])
            for u in range(2):
                nc.scalar.activation(d_sq[:, 2 * u : 2 * u + 2, :], d_ps[c][u][:], ACT.Square)
            return d_sq

        def inverse_roots(d_sq, lo, width, name, tag):
            root = held([P, PACK, width], F32, name, tag=tag)
            for t in range(PACK):
                nc.scalar.activation(
                    root[:, t, :],
                    d_sq[:, t, lo : lo + width],
                    ACT.Abs_reciprocal_sqrt,
                    bias=inv_gain[:, t : t + 1],
                    scale=inv_gain[:, t : t + 1],
                )
            return root

        out_rows = out.rearrange("(m p) j -> p m j", p=P)

        def second_stage(root, width, name, tags):
            h_b = held([P, PACK * width], BF16, name + "_b")
            for lo in range(0, width, P):
                src = planes(root[:, :, lo : lo + P])
                nc.vector.tensor_tensor(interleaved(h_b[:, PACK * lo : PACK * (lo + P)]), src, src, ALU.mult)
            if width > P:
                h_q, h_s = quantise_halves(h_b, width, name)
            else:
                h_q, h_s = quantise(h_b[:], width, name)
            banks = []
            per_bank = N // P // len(tags)
            for u, tag in enumerate(tags):
                o_ps = psum.tile([P, per_bank, width], F32, name=f"{name}_o{u}", tag=tag)
                for w in range(per_bank):
                    m = per_bank * u + w
                    nc.tensor.matmul_mx(
                        out=o_ps[:, w, :],
                        lhsT=wo_q[:, m * P : (m + 1) * P].bitcast(E4M3),
                        lhsT_scale=wo_s[:, m * P : (m + 1) * P],
                        rhs=h_q.bitcast(E4M3),
                        rhs_scale=h_s[:],
                        start=True,
                        stop=True,
                    )
                banks.append(o_ps)
            return banks

        def store(lo, width, banks, u, copy):
            per_bank = N // P // len(banks)
            staged = held([P, per_bank, width], F32, f"staged{lo}{u}")
            copy(out=staged[:], in_=banks[u][:])
            nc.sync.dma_start(out=out_rows[:, per_bank * u : per_bank * (u + 1), lo : lo + width], in_=staged[:])

        last = CHUNKS - 1
        first_stage(0, [None, None])
        for c in range(1, last):
            first_stage(c, [late_v[:, (c - 1) * CHUNK : c * CHUNK], None])
        roots = [inverse_roots(squares(c), 0, CHUNK, f"root{c}", ["x10", "x13", "wn0"][c]) for c in range(last)]

        wo_b = held([P, PACK * N], BF16, "wo_b", tag="wnb0")
        for lo in range(0, N, N // 2):
            nc.vector.tensor_copy(
                out=interleaved(wo_b[:, PACK * lo : PACK * (lo + N // 2)]), in_=planes(wo_sb[:, :, lo : lo + N // 2])
            )
        wo_q, wo_s = quantise_halves(wo_b, N, "woq")

        vec, sca = nc.vector.tensor_copy, nc.scalar.copy
        banks = [second_stage(roots[0], CHUNK, "h0", ["bank00", "bank01"])]
        for u in range(2):
            store(0, CHUNK, banks[0], u, sca)
        last_v = held([P, PASSES, CHUNK], U32, "last_v", tag="x10")
        first_stage(last, [last_v[:, a, :] for a in range(PASSES)])
        last_sq = squares(last)
        last_roots = [inverse_roots(last_sq, lo, P, f"root{last}{lo}", tag) for lo, tag in ((0, "wn1"), (P, "x12"))]
        banks.append(second_stage(roots[1], CHUNK, "h1", ["bank10", "bank11"]))
        banks.append(second_stage(roots[2], CHUNK, "h2", ["bank20", "bank21"]))
        store(CHUNK, CHUNK, banks[1], 0, vec)
        first_half = second_stage(last_roots[0], P, "h30", ["bank30", "bank01"])
        second_half = second_stage(last_roots[1], P, "h31", ["bank31", "bank00"])
        store(CHUNK, CHUNK, banks[1], 1, sca)
        for u in range(2):
            store(2 * CHUNK, CHUNK, banks[2], u, sca)
        staged = held([P, N // P, CHUNK], F32, "staged_last")
        for u, copy in enumerate((vec, sca)):
            copy(out=staged[:, 2 * u : 2 * u + 2, :P], in_=first_half[u][:])
            copy(out=staged[:, 2 * u : 2 * u + 2, P:], in_=second_half[u][:])
            nc.sync.dma_start(out=out_rows[:, 2 * u : 2 * u + 2, last * CHUNK :], in_=staged[:, 2 * u : 2 * u + 2, :])
